import numpy as np, ml_dtypes
CORES = [40,41,42,43,44,45,46,47]
N = 8
BF = ml_dtypes.bfloat16
M, S, B, L, CAP, MISS, FILL, LN = 1024, 5120, 4096, 3, 160, 512, 3840, 3
def split(s):
    t = (13 * s) >> 2
    return t & (N - 1), (t >> LN) & (B - 1)
def first(c):
    k = np.ascontiguousarray(c, np.uint8).view(np.uint64); o = np.lexsort((k[:, 1], k[:, 0])); same = np.all(k[o[1:]] == k[o[:-1]], axis=1)
    m = np.ones(len(k), bool); m[o[1:][same]] = False; return m
def weights(rng, kind):
    w = 2 * rng.integers(0, 128, (8, 16)) + 1; w[:, :4] = 2 * rng.integers(64, 128, (8, 4)) + 1
    if kind == "near": return np.tile(np.repeat(np.array([109, 185]), 8), (8, 1))
    if kind == "spread": w[:, 4:] = rng.choice(np.array([1, 3, 255]), (8, 12))
    return rng.permuted(w, axis=1)
def pool(rng, n, kind):
    if kind == "spread": c = (1 + np.floor(255 * rng.random((n, 16)) ** 6)).astype(np.uint8)
    else: c = rng.integers(2, 255, (n, 16), dtype=np.uint8) if kind == "near" else rng.integers(1, 256, (n, 16), dtype=np.uint8)
    if kind != "near": c[0] = 1; c[1] = 255
    return c[first(c)]
def counts(rng, kind, top):
    cnt = np.zeros((N, N), np.int64)
    for r in range(N):
        if kind == "full":
            q = rng.permutation(N); left = M
            for e in [top] + [int(x) for x in q if x != top]:
                cnt[r, e] = min(CAP, left); left -= min(CAP, left)
        else:
            v = rng.multinomial(M, np.full(N, 2.0 ** -LN))
            while np.max(v) > CAP:
                i = np.argmax(v); e = v[i] - CAP; v[i] = CAP; v[np.argmin(v)] += e
            cnt[r] = v
    return cnt
def alter(rng, ch, wg, m):
    lift = (294 - wg).astype(np.uint8); can = ch <= 255 - lift
    u = np.flatnonzero((((13 * (ch.astype(np.int64) @ wg)) & 3) != 3) & np.any(can, axis=1))[:m // 2]
    one = ch[u]; i = np.argmax(np.where(can[u], rng.random((len(u), 16)), -1.0), axis=1); one[np.arange(len(u)), i] += lift[i]
    two = ch[:m - len(u)].copy(); a = np.arange(len(two))
    i = rng.permuted(np.tile(np.arange(8), (len(two), 1)), axis=1)[:, :2] + 8 * rng.integers(0, 2, (len(two), 1)); two[a, i[:, 0]] += 1; two[a, i[:, 1]] -= 1
    return np.concatenate([two, one])
def make(rng, kind):
    w = weights(rng, kind); chunks = np.zeros((N, 8, 16, M), np.uint8); store = np.zeros((N, 8, 16, S), np.uint8)
    head = np.zeros((N, 8, B), np.int32); follow = np.zeros((N, 8, S), np.int32); vac = np.zeros((N, 8, MISS), np.int32)
    for g in range(8):
        c = pool(rng, N * (3 * FILL // 2 + 2 * MISS), kind); own, buc = split(c.astype(np.int64) @ w[g])
        key = own * B + buc; o = np.argsort(key, kind="stable"); ks = key[o]; rk = np.zeros(len(c), np.int64); rk[o] = np.arange(len(c)) - np.searchsorted(ks, ks)
        top = int(rng.integers(0, N)); cnt = counts(rng, kind, top); parts = [[] for r in range(N)]; stored = np.zeros(len(c), bool)
        for q in range(N):
            mine = np.flatnonzero(own == q); st = mine[rk[mine] < L][:FILL]; stored[st] = True; rest = rng.permutation(mine[~stored[mine]])
            pl = rng.permutation(S - 1) + 1; at = pl[:FILL]; vac[q, g] = pl[FILL:FILL + MISS]; store[q, g][:, at] = c[st].T
            tab = np.zeros((B, L + 1), np.int64); tab[buc[st], rk[st]] = at; head[q, g] = tab[:, 0]; follow[q, g][at] = tab[buc[st], rk[st] + 1]
            n = int(np.sum(cnt[:, q])); h = rng.permutation(FILL)
            if kind == "full": m = MISS if q == top else int(rng.integers(0, MISS + 1))
            elif kind == "deep": m = 0 if (q + g) % 2 else int(rng.integers(1, MISS + 1))
            else: m = int(rng.integers(MISS // 4, MISS + 1))
            m = min(m, n)
            if kind == "deep":
                h = h[np.argsort(-rk[st[h]], kind="stable")]; rest = rest[np.argsort(-np.count_nonzero(tab, axis=1)[buc[rest]], kind="stable")]
            if kind == "near": new = alter(rng, c[st[h]], w[g], m)
            else: new = c[rest[:m]]
            both = np.concatenate([new, c[st[h[:n - m]]]]); e = np.add.accumulate(cnt[:, q])
            if kind == "full" and q == top: both = np.roll(both, CAP * int(rng.integers(0, N)), axis=0)
            else: both = rng.permutation(both)
            for r in range(N): parts[r].append(both[e[r] - cnt[r, q]:e[r]])
        for r in range(N): chunks[r, g] = rng.permutation(np.concatenate(parts[r])).T
    return {"chunks": chunks.reshape(N, 128, M).astype(np.float32).astype(BF), "store": store.reshape(N, 128, S).astype(np.float32).astype(BF), "head": head, "follow": follow, "vac": vac,
            "wt": np.broadcast_to(w.reshape(128, 1), (N, 128, 1)).astype(np.float32)}
def setup_inputs(rng):
    return make(rng, "plain")
def setup_inputs_full(rng):
    return make(rng, "full")
def setup_inputs_near(rng):
    return make(rng, "near")
def setup_inputs_deep(rng):
    return make(rng, "deep")
def setup_inputs_spread(rng):
    return make(rng, "spread")
def whole(v, lo, hi):
    return bool(np.all((v >= lo) & (v <= hi) & (v == np.floor(v))))
def check_inputs(d):
    c, s, w = [np.asarray(d[k]).astype(np.float32) for k in ("chunks", "store", "wt")]; head, follow, vac = [np.asarray(d[k]).astype(np.int64) for k in ("head", "follow", "vac")]; bad = []
    if not whole(w, 1, 255) or not np.all(2 * np.floor(w * 0.5) != w) or not np.all(w == w[:1]): bad.append("weights")
    if not whole(c, 1, 255): bad.append("symbols")
    if not whole(s, 0, 255): bad.append("store")
    for k, v in (("head", head), ("follow", follow), ("vac", vac)):
        if not whole(v, 0, S - 1): bad.append(k)
    if bad: return bad
    c = c.astype(np.int64).reshape(N, 8, 16, M); s = s.astype(np.int64).reshape(N, 8, 16, S); w = w[0].astype(np.int64).reshape(8, 16)
    full = np.all(s > 0, axis=2); empty = np.all(s == 0, axis=2)
    if not np.all(full | empty) or np.any(full[:, :, 0]): bad.append("store")
    if np.any(follow[empty] != 0): bad.append("follow of an empty place")
    for g in range(8):
        for q in range(N):
            so, sb = split(w[g] @ s[q, g]); p = head[q, g]; seen = np.zeros(S, np.int64); ok = True
            for step in range(L):
                b = np.flatnonzero(p > 0); e = p[b]; ok = ok and bool(np.all(full[q, g][e] & (so[e] == q) & (sb[e] == b)))
                seen += np.bincount(e, minlength=S); p = follow[q, g][p]
            if not ok or np.any(p != 0) or not np.array_equal(seen, full[q, g].astype(np.int64)): bad.append("chains")
            v = vac[q, g]
            if len(np.unique(v)) != MISS or np.any(v == 0) or not np.all(empty[q, g][v]): bad.append("vacant places")
        nc = c[:, g].transpose(0, 2, 1).reshape(-1, 16); sc = s[:, g].transpose(0, 2, 1).reshape(-1, 16)[full[:, g].reshape(-1)]
        own = split(nc @ w[g])[0]; m = first(np.concatenate([sc, nc])); miss = m[len(sc):]
        if not np.all(m[:len(sc)]): bad.append("stored chunks differ")
        if not np.all(first(nc)): bad.append("new chunks differ")
        for q in range(N):
            if np.max(np.count_nonzero(own.reshape(N, M) == q, axis=1)) > CAP: bad.append("chunks of a pair")
            if np.count_nonzero(miss & (own == q)) > MISS: bad.append("misses")
    return sorted(set(bad))
def reference(chunks, store, head, follow, vac, wt):
    y = np.zeros((N, 8, M), np.float32); z = np.array(store)
    for g in range(8):
        raw = np.ascontiguousarray(chunks[:, 16 * g:16 * g + 16].transpose(1, 0, 2)).reshape(16, N * M)
        c = raw.astype(np.float32).astype(np.int64); own, buc = split(wt[0, 16 * g:16 * g + 16, 0].astype(np.int64) @ c); res = np.zeros(N * M, np.int64)
        for q in range(N):
            st = store[q, 16 * g:16 * g + 16].astype(np.float32).astype(np.int64); j = np.flatnonzero(own == q); v = c[:, j]
            p = head[q, g][buc[j]].astype(np.int64); ans = np.zeros(len(j), np.int64)
            for step in range(L):
                ans = np.where((p > 0) & np.all(st[:, p] == v, axis=0), p, ans); p = follow[q, g][p].astype(np.int64)
            miss = np.flatnonzero(ans == 0); new = vac[q, g][:len(miss)].astype(np.int64)
            ans[miss] = new; z[q, 16 * g:16 * g + 16][:, new] = raw[:, j[miss]]
            res[j] = q * S + ans
        y[:, g] = res.reshape(N, M)
    return {"y": y, "z": z}

@@ -1,0 +1,393 @@
+from concourse.bass import DstId, RemoteDMATransfer
+from concourse.mybir import AluOpType as Op, ActivationFunctionType as Act
+
+N, M, S, B, CAP, MISS = 8, 1024, 5120, 4096, 160, 512
+R_ = N * CAP
+C_ = R_ // 16
+H_ = R_ // 2
+BC = CAP // 16
+WW = MISS + 3 * R_
+DH, DV, DF = B // 16, MISS // 16, S // 16
+DD = DH + DV + DF
+
+SCRATCH = {
+    "ch": ("sbuf", [128, M], "bfloat16"),
+    "wtc": ("sbuf", [128, 8], "float32"),
+    "st": ("sbuf", [128, S + R_], "bfloat16"),
+    "tb": ("sbuf", [128, S], "bfloat16"),
+    "di": ("sbuf", [128, DD], "int32"),
+    "df": ("sbuf", [128, DD], "float32"),
+    "hi": ("sbuf", [128, DD], "bfloat16"),
+    "lo": ("sbuf", [128, DD], "bfloat16"),
+    "sb": ("sbuf", [128, R_], "bfloat16"),
+    "rb": ("sbuf", [128, R_], "bfloat16"),
+    "w": ("sbuf", [128, WW + 16], "bfloat16"),
+    "nq": ("sbuf", [128, 3 * R_], "bfloat16"),
+    "an": ("sbuf", [128, R_], "bfloat16"),
+    "ab": ("sbuf", [128, R_], "bfloat16"),
+    "yg": ("sbuf", [128, M], "bfloat16"),
+    "g3": ("sbuf", [128, 320], "bfloat16"),
+    "ys": ("sbuf", [128, 64], "float32"),
+    "ki": ("sbuf", [128, 8], "int32"),
+    "kf": ("sbuf", [128, 8], "float32"),
+    "ci": ("sbuf", [128, 8], "int32"),
+    "cf": ("sbuf", [128, 8], "float32"),
+    "u": ("sbuf", [128, 144], "float32"),
+    "neg1": ("sbuf", [128, 128], "bfloat16"),
+    "p2n": ("sbuf", [128, 128], "bfloat16"),
+    "negu": ("sbuf", [128, 128], "bfloat16"),
+    "negb": ("sbuf", [128, 128], "bfloat16"),
+    "ident": ("sbuf", [128, 128], "bfloat16"),
+    "nid": ("sbuf", [128, 128], "bfloat16"),
+    "negi": ("sbuf", [128, 128], "float32"),
+    "sel": ("sbuf", [128, 144], "bfloat16"),
+    "sel4": ("sbuf", [128, 144], "bfloat16"),
+    "wh": ("sbuf", [128, 144], "bfloat16"),
+    "wn": ("sbuf", [128, 144], "bfloat16"),
+    "rm": ("sbuf", [128, 512], "bfloat16"),
+    "nc0": ("sbuf", [128, 3 * C_], "float32"),
+    "ncs": ("sbuf", [128, 3 * C_], "float32"),
+    "ndu": ("sbuf", [128, C_], "float32"),
+    "pz": ("sbuf", [128, C_], "float32"),
+    "npad": ("sbuf", [128, C_], "float32"),
+    "t1": ("sbuf", [128, 64], "int32"),
+    "o4": ("sbuf", [128, 64], "int32"),
+    "o160": ("sbuf", [128, 64], "bfloat16"),
+    "e1": ("sbuf", [128, 512], "bfloat16"),
+    "s1": ("sbuf", [128, 512], "bfloat16"),
+    "pr": ("sbuf", [128, 512], "bfloat16"),
+    "pos": ("sbuf", [128, 64], "uint16"),
+    "t2": ("sbuf", [128, C_], "int32"),
+    "b2": ("sbuf", [128, C_], "int32"),
+    "lu": ("sbuf", [128, 4 * C_], "uint16"),
+    "mm": ("sbuf", [128, C_], "float32"),
+    "m3": ("sbuf", [128, C_], "float32"),
+    "thr": ("sbuf", [128, C_], "float32"),
+    "e2": ("sbuf", [128, C_], "bfloat16"),
+    "s2": ("sbuf", [128, C_], "bfloat16"),
+    "xf": ("sbuf", [128, C_], "float32"),
+    "idx": ("sbuf", [128, C_], "uint16"),
+    "tg": ("sbuf", [128, C_], "uint16"),
+}
+for _k in range(8):
+    SCRATCH["ps%d" % _k] = ("psum", [128, 512], "float32")
+
+SEMAPHORES = ["sv", "sa", "sp", "sg", "l_ch", "l_wt", "l_h", "l_fv", "l_st", "rl",
+              "arr1", "snt1", "arr2", "snt2", "oz", "oy"]
+
+
+def rank_program(g, core, T, topo):
+    me = T.rank_of(core)
+    if me is None:
+        return
+    sem = T.sem
+    V, A, P, Y = g.vector, g.scalar, g.tensor, g.sync
+    cnt = {"sv": 0, "sa": 0, "sp": 0, "sg": 0}
+    seen = {}
+
+    def done(inst, name):
+        inst.then_inc(sem[name], 1)
+        cnt[name] += 1
+        return (name, cnt[name])
+
+    def wait(q, qn, *toks):
+        for name, n in toks:
+            if seen.get((qn, name), 0) < n:
+                q.wait_ge(sem[name], n)
+                seen[(qn, name)] = n
+
+    def v(inst_fn, *toks):
+        wait(V, "v", *toks)
+        return done(inst_fn(), "sv")
+
+    def a(inst_fn, *toks):
+        wait(A, "a", *toks)
+        return done(inst_fn(), "sa")
+
+    def gp(inst_fn, *toks):
+        wait(g, "g", *toks)
+        return done(inst_fn(), "sg")
+
+    def conv(out, lhs, rhs_of, start=True, lo=0, hi=16):
+        inst = None
+        for i in range(lo, hi):
+            inst = P.matmul(out, lhs[:, 15 - i:143 - i], rhs_of(i), start and i == 0, i == 15)
+        return inst
+
+    ps = [T["ps%d" % k] for k in range(8)]
+    peers = [r for r in range(N) if r != me]
+    far = [r for r in peers if topo.die(T.cores[r]) != topo.die(core)]
+    near = [r for r in peers if topo.die(T.cores[r]) == topo.die(core)]
+    fc = BC * min(far)
+    nc = BC * min(near + [me])
+
+    def dst_id(r):
+        rid, pid, _ = topo.addr(T.cores[r])
+        return DstId(rid=rid, pnc=pid)
+
+    def bits(es):
+        m = 0
+        for e in es:
+            m |= 1 << e
+        return m
+
+    Y.dma_start(T.ch[:], T.chunks[:]).then_inc(sem.l_ch, 16)
+    A.dma_start(T.wtc[:, 0:1], T.wt[:]).then_inc(sem.l_wt, 16)
+    Y.dma_start(T.di[:, 0:DH], T.head[:]).then_inc(sem.l_h, 16)
+    Y.dma_start(T.di[:, DH:DH + DV], T.vac[:]).then_inc(sem.l_fv, 16)
+    Y.dma_start(T.di[:, DH + DV:DD], T.follow[:]).then_inc(sem.l_fv, 16)
+    Y.dma_start(T.st[:, 0:S], T.store[:]).then_inc(sem.l_st, 16)
+    L_CH, L_WT, L_H, L_FV, L_ST = ("l_ch", 16), ("l_wt", 16), ("l_h", 16), ("l_fv", 32), ("l_st", 16)
+
+    fl = {"allow_small_or_imprecise_dtypes": True}
+    g_k = gp(lambda: g.iota(T.ki[:, 0:1], [[0, 1]], 0, 1))
+    g_u = gp(lambda: g.iota(T.u[:], [[1, 144]], 0, 0, **fl))
+    g_kf = gp(lambda: g.iota(T.kf[:, 0:1], [[0, 1]], 0, 1, **fl))
+    g_n1 = gp(lambda: g.iota(T.neg1[:], [[0, 128]], -1, 0, **fl))
+    g_p2 = gp(lambda: g.affine_select(T.p2n[:], T.neg1[:], [[16, 8], [0, 16]], Op.is_ge, 0.0, 15, -1), g_n1)
+    g_nu = gp(lambda: g.affine_select(T.negu[:], T.p2n[:], [[-1, 128]], Op.is_ge, 0.0, 0, 1), g_p2)
+    g_nb = gp(lambda: g.affine_select(T.negb[:], T.p2n[:], [[-16, 8], [0, 16]], Op.is_ge, 0.0, 0, 1))
+    g_wz = gp(lambda: g.iota(T.w[:, 0:MISS], [[0, MISS]], 0, 0, **fl))
+    g_nc = gp(lambda: g.iota(T.nc0[:], [[-16, 3 * C_]], -MISS, 0, **fl))
+    g_zc = gp(lambda: g.iota(T.w[:, WW:WW + 16], [[0, 16]], 0, 0, **fl))
+
+    v_tz = v(lambda: V.memset(T.tb[:, 0:2048], 0.0))
+    v_g = v(lambda: V.tensor_scalar(T.ci[:, 0:1], T.ki[:, 0:1], 112, None, Op.bitwise_and), g_k)
+    v_sb = v(lambda: V.memset(T.sb[:], 0.0))
+    v_gf = v(lambda: V.tensor_scalar(T.cf[:, 0:1], T.ci[:, 0:1], 15.0, None, Op.add), v_g)
+    v_r1 = v(lambda: V.memset(T.rm[:], 1.0))
+    v_id = v(lambda: V.tensor_scalar(T.ident[:], T.u[:, 0:128], T.kf[:, 0:1], None, Op.is_equal), g_kf)
+    v_rm = v(lambda: V.memset(T.rm[:, 0:512:64], 0.0), v_r1)
+    v_wh = v(lambda: V.tensor_scalar(T.wh[:], T.u[:], T.cf[:, 0:1], T.wtc[:, 0:1], Op.is_equal, Op.mult), v_gf, L_WT)
+    v_sel = v(lambda: V.tensor_scalar(T.sel[:], T.u[:], T.cf[:, 0:1], None, Op.is_equal))
+    v_ni = v(lambda: V.tensor_scalar(T.negi[:], T.u[:, 0:128], T.kf[:, 0:1], -1.0, Op.is_equal, Op.mult))
+
+    a(lambda: A.activation(T.tb[:, 2048:4096], T.tb[:, 0:2048], Act.Copy), v_tz)
+    a(lambda: A.activation(T.tb[:, 4096:S], T.tb[:, 0:1024], Act.Copy))
+    a(lambda: A.activation(T.nid[:], T.ident[:], Act.Copy, scale=-1.0), v_id)
+    a_wn = a(lambda: A.activation(T.wn[:], T.sel[:], Act.Copy, scale=-8192.0), v_sel)
+
+    wait(P, "p", v_wh, L_CH)
+    p_h1 = done(conv(ps[5][:, 0:64], T.wh, lambda i: T.ch[:, i:M:16]), "sp")
+    v_t1 = v(lambda: V.tensor_scalar(T.t1[:], ps[5][:, 0:64], 13.0, None, Op.mult), p_h1)
+    v_o4 = v(lambda: V.tensor_scalar(T.o4[:], T.t1[:], 28, None, Op.bitwise_and), v_t1)
+    v_e = None
+    for q in range(N):
+        v_e = v(lambda: V.tensor_scalar(T.e1[:, 64 * q:64 * q + 64], T.o4[:], float(4 * q), None, Op.is_equal), v_o4)
+    v_s1 = v(lambda: V.tensor_tensor_scan(T.s1[:], T.rm[:], T.e1[:], 0.0, Op.mult, Op.subtract), v_e, v_rm)
+    wait(P, "p", v_e, g_nu)
+    P.matmul(ps[6][:, 0:512], T.negu[:], T.e1[:], True, False)
+    wait(P, "p", v_s1, g_nb)
+    p_n1 = done(P.matmul(ps[6][:, 0:512], T.negb[:], T.s1[:], False, True), "sp")
+    v_o160 = v(lambda: V.tensor_scalar(T.o160[:], T.o4[:], 40.0, None, Op.mult))
+    v_d1 = v(lambda: V.tensor_copy(T.df[:, 0:DH], T.di[:, 0:DH]), L_H)
+    v_pr = v(lambda: V.tensor_tensor(T.pr[:], ps[6][:, 0:512], T.e1[:], Op.mult), p_n1)
+    wait(P, "p", v_o160, v_id)
+    P.matmul(ps[7][:, 0:64], T.ident[:], T.o160[:], True, False)
+    wait(P, "p", v_pr)
+    inst = None
+    for q in range(N):
+        inst = P.matmul(ps[7][:, 0:64], T.ident[:], T.pr[:, 64 * q:64 * q + 64], False, q == N - 1)
+    p_sum = done(inst, "sp")
+    v_d2 = v(lambda: V.tensor_copy(T.df[:, DH:DD], T.di[:, DH:DD]), L_FV)
+    v_pos = v(lambda: V.tensor_copy(T.pos[:], ps[7][:, 0:64]), p_sum)
+    v_sc0 = v(lambda: V.tensor_copy(T.sb[:].indirect(T.pos[:]), T.ch[:]), v_pos, v_sb)
+
+    eng = topo.engines(core, T.cores[peers[0]])
+    ev, od = eng[0::2], eng[1::2]
+    tr = []
+    for n_, r in enumerate(far):
+        tr.append((r, ev[2 * n_:2 * n_ + 2]))
+    for n_, r in enumerate(near):
+        tr.append((r, od[2 * n_:2 * n_ + 2]))
+    wait(g, "g", v_sc0)
+    g.remote_dma_fused([RemoteDMATransfer(dst_ids=[dst_id(r)], dma_engine_mask=bits(es), remote_sem=sem.arr1,
+                                          src=T.sb[:, CAP * r:CAP * r + CAP], dst=T.rb[:, CAP * me:CAP * me + CAP])
+                        for r, es in tr], local_sem=sem.snt1)
+    ARR1 = ("arr1", 2 * len(peers))
+
+    a_h1 = a(lambda: A.activation(T.hi[:, 0:DH], T.df[:, 0:DH], Act.Copy), v_d1)
+    a_h2 = a(lambda: A.activation(T.hi[:, DH:DD], T.df[:, DH:DD], Act.Copy), v_d2)
+    wait(P, "p", v_ni, a_h1)
+    P.matmul(ps[2][:, 0:DH], T.negi[:], T.df[:, 0:DH], True, False)
+    p_l1 = done(P.matmul(ps[2][:, 0:DH], T.ident[:], T.hi[:, 0:DH], False, True), "sp")
+    wait(P, "p", a_h2)
+    P.matmul(ps[3][:, 0:DD - DH], T.negi[:], T.df[:, DH:DD], True, False)
+    p_l2 = done(P.matmul(ps[3][:, 0:DD - DH], T.ident[:], T.hi[:, DH:DD], False, True), "sp")
+    a_l1 = a(lambda: A.activation(T.lo[:, 0:DH], ps[2][:, 0:DH], Act.Copy, scale=-1.0), p_l1)
+    a_l2 = a(lambda: A.activation(T.lo[:, DH:DD], ps[3][:, 0:DD - DH], Act.Copy, scale=-1.0), p_l2)
+    wait(Y, "y", a_h2, g_wz)
+    Y.dma_start(T.tb[0:128:16, 0:B], T.hi[:, 0:DH]).then_inc(sem.rl, 16)
+    Y.dma_start(T.tb[2:128:16, 0:S], T.hi[:, DH + DV:DD]).then_inc(sem.rl, 16)
+    Y.dma_start(T.w[0:128:16, 0:MISS], T.hi[:, DH:DH + DV]).then_inc(sem.rl, 16)
+    wait(Y, "y", a_l1)
+    Y.dma_start(T.tb[1:128:16, 0:B], T.lo[:, 0:DH]).then_inc(sem.rl, 16)
+    wait(Y, "y", a_l2)
+    Y.dma_start(T.tb[3:128:16, 0:S], T.lo[:, DH + DV:DD]).then_inc(sem.rl, 16)
+    Y.dma_start(T.w[1:128:16, 0:MISS], T.lo[:, DH:DH + DV]).then_inc(sem.rl, 16)
+    RL = ("rl", 96)
+    a_own = a(lambda: A.activation(T.rb[:, CAP * me:CAP * me + CAP], T.sb[:, CAP * me:CAP * me + CAP], Act.Copy), v_sc0)
+
+    v_r = v(lambda: V.tensor_scalar(T.ci[:, 4:5], T.ki[:, 0:1], 15, None, Op.bitwise_and))
+    v_rf = v(lambda: V.tensor_copy(T.cf[:, 1:2], T.ci[:, 4:5]), v_r)
+    v(lambda: V.tensor_scalar(T.cf[:, 2:3], T.ci[:, 4:5], 2.0, None, Op.is_lt))
+    v(lambda: V.tensor_scalar(T.cf[:, 3:4], T.ci[:, 4:5], 2.0, None, Op.is_ge))
+    v(lambda: V.tensor_scalar(T.cf[:, 4:5], T.ci[:, 4:5], 4.0, float(S * me), Op.is_equal, Op.mult))
+    v_m4 = v(lambda: V.tensor_scalar(T.cf[:, 5:6], T.ci[:, 4:5], 4.0, None, Op.is_lt))
+    v(lambda: V.tensor_scalar(T.ncs[:], T.nc0[:], T.cf[:, 1:2], None, Op.subtract), v_rf, g_zc)
+    v(lambda: V.tensor_scalar(T.ndu[:], T.nc0[:, 0:C_], T.cf[:, 1:2], float(MISS - S), Op.subtract, Op.add))
+    v(lambda: V.tensor_scalar(T.sel4[:], T.u[:], T.cf[:, 0:1], T.cf[:, 5:6], Op.is_equal, Op.mult), v_m4)
+    mH, mF, bias = T.cf[:, 2:3], T.cf[:, 3:4], T.cf[:, 4:5]
+    st = T.st[:, 0:S]
+
+    wait(P, "p", a_own, ARR1)
+    p_h2 = done(conv(ps[5][:, 0:C_], T.wh, lambda i: T.rb[:, i:R_:16]), "sp")
+    v_t2 = v(lambda: V.tensor_scalar(T.t2[:], ps[5][:, 0:C_], 13.0, None, Op.mult), p_h2)
+    v_b2 = v(lambda: V.tensor_scalar(T.b2[:], T.t2[:], 5, B - 1, Op.arith_shift_right, Op.bitwise_and), v_t2)
+    v_l0 = v(lambda: V.tensor_copy(T.lu[:, 0:C_], T.b2[:]), v_b2)
+
+    def gout(k, c0, c1):
+        return T.w[:, MISS + R_ * k + 16 * c0:MISS + R_ * k + 16 * c1]
+
+    def a_gather(k, c0, c1, width, mask, *toks):
+        return a(lambda: A.activation(gout(k, c0, c1), T.tb[:, 0:width].indirect(T.lu[:, C_ * k + c0:C_ * k + c1]),
+                                      Act.Copy, scale=mask), *toks)
+
+    def v_head(c0, c1, *toks):
+        return v(lambda: V.tensor_scalar(gout(0, c0, c1), T.tb[:, 0:B].indirect(T.lu[:, c0:c1]), mH, None, Op.mult), *toks)
+
+    def p_list(k, h, *toks):
+        wait(P, "p", *toks)
+        b0 = MISS + R_ * k + H_ * h
+        return done(conv(ps[h][:, 0:40], T.sel, lambda i: T.w[:, b0 + i:b0 + H_:16]), "sp")
+
+    def v_list(k, h, tok):
+        c0 = C_ * (k + 1) + 40 * h
+        return v(lambda: V.tensor_copy(T.lu[:, c0:c0 + 40], ps[h][:, 0:40]), tok)
+
+    def v_cmp(k, c0, c1, *toks):
+        l0 = C_ * (k + 1)
+        b0 = R_ * k
+        return v(lambda: V.tensor_tensor(T.nq[:, b0 + 16 * c0:b0 + 16 * c1], st.indirect(T.lu[:, l0 + c0:l0 + c1]),
+                                         T.rb[:, 16 * c0:16 * c1], Op.not_equal), *toks)
+
+    def p_match(k, *toks):
+        out = ps[2 + k][:, 0:C_]
+        P.matmul(out, T.negi[:], T.ncs[:, C_ * k:C_ * k + C_], True, False)
+        wait(P, "p", *toks)
+        b0 = R_ * k
+        return done(conv(out, T.wn, lambda i: T.nq[:, b0 + i:b0 + R_:16], start=False), "sp")
+
+    a_ha = a_gather(0, 0, 20, B, mH, v_l0, RL)
+    a_hb = a_gather(0, 56, 80, B, mH)
+    v_ha = v_head(20, 40, v_l0, RL)
+    v_hb = v_head(40, 56)
+    v_m0 = v(lambda: V.tensor_scalar(T.mm[:], T.t2[:], -32.0, float(WW), Op.mult, Op.add))
+    v_pz = v(lambda: V.tensor_scalar(T.pz[:], T.t2[:], 0.0, None, Op.is_equal))
+    p1a = p_list(0, 0, a_ha, v_ha)
+    p1b = p_list(0, 1, a_hb, v_hb)
+    l1a = v_list(0, 0, p1a)
+    c1a = v_cmp(0, 0, 40, l1a, L_ST, ARR1, a_own)
+    l1b = v_list(0, 1, p1b)
+    c1b = v_cmp(0, 40, 80, l1b)
+    f1a = a_gather(1, 0, 40, S, mF, l1a)
+    f1b = a_gather(1, 40, 80, S, mF, l1b)
+    p2a = p_list(1, 0, f1a)
+    p2b = p_list(1, 1, f1b)
+    x1 = p_match(0, c1b)
+    l2a = v_list(1, 0, p2a)
+    c2a = v_cmp(1, 0, 40, l2a)
+    l2b = v_list(1, 1, p2b)
+    c2b = v_cmp(1, 40, 80, l2b)
+    f2a = a_gather(2, 0, 40, S, mF, l2a)
+    f2b = a_gather(2, 40, 80, S, mF, l2b)
+    p3a = p_list(2, 0, f2a)
+    p3b = p_list(2, 1, f2b)
+    l3a = v_list(2, 0, p3a)
+    c3a = v_cmp(2, 0, 20, l3a)
+    l3b = v_list(2, 1, p3b)
+    c3b = v_cmp(2, 40, 80, l3b)
+    a_g3 = a(lambda: A.activation(T.g3[:], st.indirect(T.lu[:, 3 * C_ + 20:3 * C_ + 40]), Act.Copy), l3a)
+    wait(P, "p", a_g3)
+    P.matmul(ps[7][:, 0:320], T.nid[:], T.rb[:, 320:640], True, False)
+    p_d3 = done(P.matmul(ps[7][:, 0:320], T.ident[:], T.g3[:], False, True), "sp")
+    a_d3 = a(lambda: A.activation(T.nq[:, 2 * R_ + 320:2 * R_ + 640], ps[7][:, 0:320], Act.Abs), p_d3)
+    x2 = p_match(1, c2b)
+    x3 = p_match(2, a_d3, c3b)
+
+    v_m1 = v(lambda: V.tensor_tensor(T.m3[:], ps[2][:, 0:C_], T.mm[:], Op.max), x1, v_m0)
+    v_np = v(lambda: V.tensor_tensor(T.npad[:], T.pz[:], T.ndu[:], Op.mult), v_pz)
+    v_m2 = v(lambda: V.tensor_tensor(T.mm[:], ps[3][:, 0:C_], T.m3[:], Op.max), x2, v_m1)
+    v_th = v(lambda: V.tensor_scalar(T.thr[:], T.mm[:], -100000.0, 0.0, Op.mult, Op.min), v_m2)
+    v_e2 = v(lambda: V.tensor_tensor(T.e2[:], ps[4][:, 0:C_], T.thr[:], Op.is_lt), x3, v_th)
+    v_s2 = v(lambda: V.tensor_tensor_scan(T.s2[:], T.e2[:], T.e2[:], 0.0, Op.min, Op.subtract), v_e2)
+    v_m3 = v(lambda: V.tensor_tensor(T.m3[:], ps[4][:, 0:C_], T.mm[:], Op.max))
+    wait(P, "p", v_e2)
+    P.matmul(ps[6][:, 0:C_], T.negu[:], T.e2[:], True, False)
+    wait(P, "p", v_s2)
+    p_n2 = done(P.matmul(ps[6][:, 0:C_], T.negb[:], T.s2[:], False, True), "sp")
+    v_xf = v(lambda: V.tensor_tensor(T.xf[:], ps[6][:, 0:C_], T.m3[:], Op.max), p_n2, v_m3)
+    v_ix = v(lambda: V.tensor_copy(T.idx[:], T.xf[:]), v_xf)
+
+    def a_ans(c0, c1, *toks):
+        return a(lambda: A.activation(T.an[:, 16 * c0:16 * c1], T.w[:].indirect(T.idx[:, c0:c1]), Act.Identity,
+                                      bias=bias), *toks)
+
+    def v_ans(c0, c1, *toks):
+        return v(lambda: V.tensor_scalar(T.an[:, 16 * c0:16 * c1], T.w[:].indirect(T.idx[:, c0:c1]), bias, None, Op.add),
+                 *toks)
+
+    def p_target(bank, c0, c1, *toks):
+        out = ps[bank][:, 0:c1 - c0]
+        P.matmul(out, T.negi[:], T.npad[:, c0:c1], True, False)
+        wait(P, "p", *toks)
+        return done(conv(out, T.sel4, lambda i: T.an[:, 16 * c0 + i:16 * c1:16], start=False), "sp")
+
+    def v_fill(bank, c0, c1, tok, *prev):
+        t = v(lambda: V.tensor_copy(T.tg[:, c0:c1], ps[bank][:, 0:c1 - c0]), tok)
+        return v(lambda: V.tensor_copy(T.st[:].indirect(T.tg[:, c0:c1]), T.rb[:, 16 * c0:16 * c1]), t, *prev)
+
+    def send_answers(grp, *toks):
+        wait(g, "g", *toks)
+        g.remote_dma_fused([RemoteDMATransfer(dst_ids=[dst_id(r)], dma_engine_mask=bits(eng[4 * n_:4 * n_ + 4]),
+                                              remote_sem=sem.arr2, src=T.an[:, CAP * r:CAP * r + CAP],
+                                              dst=T.ab[:, CAP * me:CAP * me + CAP])
+                            for n_, r in enumerate(grp)], local_sem=sem.snt2)
+
+    a1 = a_ans(fc, fc + 8, v_ix, g_zc)
+    v1 = v_ans(fc + 8, fc + 16, v_ix)
+    a2 = a_ans(fc + 16, fc + 28)
+    v2 = v_ans(fc + 28, fc + 40)
+    a3 = a_ans(nc, nc + 40)
+    a_ab = a(lambda: A.activation(T.ab[:, CAP * me:CAP * me + CAP], T.an[:, CAP * me:CAP * me + CAP], Act.Copy), a3)
+    send_answers(far, a2, v2)
+    send_answers(near, a3)
+    ARR2 = ("arr2", 4 * len(peers))
+    t1_ = p_target(0, fc, fc + 16, a1, v1)
+    t2_ = p_target(1, fc + 16, fc + 40, a2, v2)
+    t3_ = p_target(2, nc, nc + 40, a3)
+    s1_ = v_fill(0, fc, fc + 16, t1_)
+    s2_ = v_fill(1, fc + 16, fc + 40, t2_, s1_)
+    s3_ = v_fill(2, nc, nc + 40, t3_, s2_)
+    wait(Y, "y", s3_)
+    Y.dma_start(T.z[:], st).then_inc(sem.oz, 16)
+
+    ya = []
+    for c0, c1 in ((0, 16), (16, 32)):
+        ya.append(a(lambda: A.activation(T.yg[:, 16 * c0:16 * c1], T.ab[:].indirect(T.pos[:, c0:c1]), Act.Copy),
+                    a_ab, ARR2))
+    yv = v(lambda: V.tensor_copy(T.yg[:, 512:M], T.ab[:].indirect(T.pos[:, 32:64])), a_ab, ARR2)
+    rhs_y = lambda i: T.yg[:, 64 * i:64 * i + 64]
+    wait(P, "p", ya[0])
+    conv(ps[5][:, 0:64], T.sel, rhs_y, lo=0, hi=4)
+    wait(P, "p", ya[1])
+    conv(ps[5][:, 0:64], T.sel, rhs_y, lo=4, hi=8)
+    wait(P, "p", yv)
+    p_y = done(conv(ps[5][:, 0:64], T.sel, rhs_y, lo=8, hi=16), "sp")
+    a_y = a(lambda: A.activation(T.ys[:], ps[5][:, 0:64], Act.Copy), p_y)
+    wait(A, "a", a_y)
+    A.dma_start(T.y[:], T.ys[:]).then_inc(sem.oy, 16)
+    A.wait_ge(sem.oy, 16)
+    Y.wait_ge(sem.oz, 16)
+    g.wait_ge(sem.snt1, 2 * len(peers))
+    g.wait_ge(sem.snt2, 4 * len(peers))

@@ -5,66 +5,92 @@ N, M, S, B, CAP, MISS = 8, 1024, 5120, 4096, 160, 512
 R_ = N * CAP
 C_ = R_ // 16
 H_ = R_ // 2
-BC = CAP // 16
-WW = MISS + 3 * R_
-DH, DV, DF = B // 16, MISS // 16, S // 16
-DD = DH + DV + DF
+HC = C_ // 2
+WW = MISS + 3 * H_
+WH = WW + 16
+WY = WH - MISS
+DH, DF = B // 16, S // 16
+DD = DH + DF
+S0 = 3072
+EP = M // 16 + 1
+BIG = 2048.0
+EPS = 2.0 ** 19
 
 SCRATCH = {
     "ch": ("sbuf", [128, M], "bfloat16"),
-    "wtc": ("sbuf", [128, 8], "float32"),
-    "st": ("sbuf", [128, S + R_], "bfloat16"),
+    "wr": ("sbuf", [128, 128], "float32"),
+    "st": ("sbuf", [128, S], "bfloat16"),
+    "zs": ("sbuf", [128, 3 * (WW + WY + H_)], "bfloat16"),
     "tb": ("sbuf", [128, S], "bfloat16"),
+    "tb2": ("sbuf", [128, B], "bfloat16"),
+    "lh": ("sbuf", [128, DH], "uint16"),
     "di": ("sbuf", [128, DD], "int32"),
-    "df": ("sbuf", [128, DD], "float32"),
-    "hi": ("sbuf", [128, DD], "bfloat16"),
-    "lo": ("sbuf", [128, DD], "bfloat16"),
+    "df": ("sbuf", [128, DF], "float32"),
+    "idf": ("sbuf", [128, DF], "float32"),
+    "hi": ("sbuf", [128, 2 * DF], "bfloat16"),
+    "lo": ("sbuf", [128, 2 * DF], "bfloat16"),
+    "b3": ("sbuf", [128, C_], "int32"),
+    "b4": ("sbuf", [128, C_], "float32"),
+    "vi": ("sbuf", [128, MISS], "int32"),
+    "vf": ("sbuf", [128, MISS], "float32"),
+    "vh": ("sbuf", [128, MISS], "bfloat16"),
+    "la": ("sbuf", [128, 128], "float32"),
+    "lb": ("sbuf", [128, 128], "bfloat16"),
+    "lc": ("sbuf", [128, 128], "bfloat16"),
     "sb": ("sbuf", [128, R_], "bfloat16"),
     "rb": ("sbuf", [128, R_], "bfloat16"),
-    "w": ("sbuf", [128, WW + 16], "bfloat16"),
+    "w": ("sbuf", [128, WH + WY], "bfloat16"),
     "nq": ("sbuf", [128, 3 * R_], "bfloat16"),
+    "n3": ("sbuf", [128, H_], "bfloat16"),
     "an": ("sbuf", [128, R_], "bfloat16"),
     "ab": ("sbuf", [128, R_], "bfloat16"),
     "yg": ("sbuf", [128, M], "bfloat16"),
-    "g3": ("sbuf", [128, 320], "bfloat16"),
-    "ys": ("sbuf", [128, 64], "float32"),
+    "ys": ("sbuf", [128, 256], "float32"),
     "ki": ("sbuf", [128, 8], "int32"),
     "kf": ("sbuf", [128, 8], "float32"),
     "ci": ("sbuf", [128, 8], "int32"),
-    "cf": ("sbuf", [128, 8], "float32"),
+    "cj": ("sbuf", [128, 8], "int32"),
+    "cf": ("sbuf", [128, 16], "float32"),
+    "below": ("sbuf", [128, 16], "float32"),
     "u": ("sbuf", [128, 144], "float32"),
-    "neg1": ("sbuf", [128, 128], "bfloat16"),
-    "p2n": ("sbuf", [128, 128], "bfloat16"),
-    "negu": ("sbuf", [128, 128], "bfloat16"),
-    "negb": ("sbuf", [128, 128], "bfloat16"),
+    "ones": ("sbuf", [128, 128], "bfloat16"),
+    "b1": ("sbuf", [128, 128], "bfloat16"),
+    "blk": ("sbuf", [128, 128], "bfloat16"),
+    "low": ("sbuf", [128, 128], "bfloat16"),
+    "lift": ("sbuf", [128, 128], "bfloat16"),
     "ident": ("sbuf", [128, 128], "bfloat16"),
-    "nid": ("sbuf", [128, 128], "bfloat16"),
     "negi": ("sbuf", [128, 128], "float32"),
+    "pos3": ("sbuf", [128, 128], "float32"),
+    "pk": ("sbuf", [128, 512], "bfloat16"),
     "sel": ("sbuf", [128, 144], "bfloat16"),
     "sel4": ("sbuf", [128, 144], "bfloat16"),
+    "sel6": ("sbuf", [128, 144], "bfloat16"),
+    "sel01": ("sbuf", [128, 144], "bfloat16"),
+    "sel23": ("sbuf", [128, 144], "bfloat16"),
+    "sely": ("sbuf", [128, 48], "bfloat16"),
     "wh": ("sbuf", [128, 144], "bfloat16"),
     "wn": ("sbuf", [128, 144], "bfloat16"),
-    "rm": ("sbuf", [128, 512], "bfloat16"),
-    "nc0": ("sbuf", [128, 3 * C_], "float32"),
-    "ncs": ("sbuf", [128, 3 * C_], "float32"),
-    "ndu": ("sbuf", [128, C_], "float32"),
-    "pz": ("sbuf", [128, C_], "float32"),
-    "npad": ("sbuf", [128, C_], "float32"),
+    "wp": ("sbuf", [128, 288], "bfloat16"),
+    "rm": ("sbuf", [128, N * EP], "bfloat16"),
+    "r8": ("sbuf", [128, 512], "bfloat16"),
+    "cap": ("sbuf", [128, 4 * C_], "float32"),
+    "np": ("sbuf", [128, R_, 2], "bfloat16"),
+    "nc0": ("sbuf", [128, 4 * HC], "float32"),
+    "ncs": ("sbuf", [128, 4 * HC], "float32"),
+    "ncy": ("sbuf", [128, 4 * HC], "bfloat16"),
+    "eps": ("sbuf", [128, HC], "float32"),
     "t1": ("sbuf", [128, 64], "int32"),
     "o4": ("sbuf", [128, 64], "int32"),
-    "o160": ("sbuf", [128, 64], "bfloat16"),
-    "e1": ("sbuf", [128, 512], "bfloat16"),
-    "s1": ("sbuf", [128, 512], "bfloat16"),
-    "pr": ("sbuf", [128, 512], "bfloat16"),
+    "e1": ("sbuf", [128, N * EP], "bfloat16"),
+    "s1": ("sbuf", [128, N * EP], "bfloat16"),
+    "px": ("sbuf", [128, 512], "float32"),
     "pos": ("sbuf", [128, 64], "uint16"),
     "t2": ("sbuf", [128, C_], "int32"),
     "b2": ("sbuf", [128, C_], "int32"),
     "lu": ("sbuf", [128, 4 * C_], "uint16"),
-    "mm": ("sbuf", [128, C_], "float32"),
-    "m3": ("sbuf", [128, C_], "float32"),
-    "thr": ("sbuf", [128, C_], "float32"),
+    "mf": ("sbuf", [128, 4 * C_], "float32"),
     "e2": ("sbuf", [128, C_], "bfloat16"),
-    "s2": ("sbuf", [128, C_], "bfloat16"),
+    "s2": ("sbuf", [128, C_ + 8], "bfloat16"),
     "xf": ("sbuf", [128, C_], "float32"),
     "idx": ("sbuf", [128, C_], "uint16"),
     "tg": ("sbuf", [128, C_], "uint16"),
@@ -72,322 +98,373 @@ SCRATCH = {
 for _k in range(8):
     SCRATCH["ps%d" % _k] = ("psum", [128, 512], "float32")
 
-SEMAPHORES = ["sv", "sa", "sp", "sg", "l_ch", "l_wt", "l_h", "l_fv", "l_st", "rl",
-              "arr1", "snt1", "arr2", "snt2", "oz", "oy"]
+SEMAPHORES = ["sv", "sa", "sp", "sg", "l_ch", "l_wt", "l_h", "l_t", "l_v", "l_st", "l_z", "rows",
+              "arr_near", "arr_far", "snt1", "arr2", "snt2", "oz", "oy"]
+
+YV = "v"
+FIRST = {0: 40, 1: 40}
+BY_SCALAR = {0: {"1Y": 7, "3Y": 4}, 1: {"1Y": 4, "3Y": 7}}
+ORDER = {
+    0: {"v": "tX bX aX jX tY l0X aY bY G0Xb jY l0Y G0Yb l2X l1X C1Xa l2Y C1Xb C2Xb l1Y l3X C2Xa C3Xa l3Y C3Xb C2Ya WX "
+             "MX eX sX C2Yb xX iX AXb MY eY sY TX xY iY SX TY SY",
+        "a": "mmX G0Xa mmY vac G0Ya G2X G2Y D1Y D3Y E1Y E3Y AXa WY ab AY",
+        "p": "hX hY c2X c1X c2Y _r1Y c1Y c3X _r3Y c3Y m2X d1Y m3X d3Y m1Y _raX _tpX rbX m3Y m2Y ctX _tpY _raY rbY ctY"},
+    1: {"v": "tY bY aY jY tX l0Y bX aX G0Ya jX l0X G0Xa l2Y C2Y l2X l1Y l1X C2X C1Xb l3Y C1Xa l3X C3X "
+             "MX eX sX WX MY xX eY iX sY AXb xY iY TX SX TY SY",
+        "a": "mmY G0Yb mmX vac G0Xb G2Y G2X D1Y D3Y E1Y E3Y WY AXa AY ab",
+        "p": "hY hX _r1Y c2Y c1Y c2X c1X _r3Y c3Y c3X m2Y d1Y m2X d3Y m3X m1Y m3Y _raX rbX _tpX _raY rbY ctX _tpY ctY"},
+}
+SECOND = (("P0", "a", 0, 96), ("P1", "a", 96, 200), ("P3", "v", 200, 256))
 
 
 def rank_program(g, core, T, topo):
     me = T.rank_of(core)
     if me is None:
         return
+    ON_SCALAR = BY_SCALAR[me // 4]
     sem = T.sem
     V, A, P, Y = g.vector, g.scalar, g.tensor, g.sync
-    cnt = {"sv": 0, "sa": 0, "sp": 0, "sg": 0}
-    seen = {}
+    queue = {"v": V, "a": A, "p": P, "g": g, "y": Y}
+    tasks, order = {}, {q: [] for q in queue}
+    landed = {}
 
-    def done(inst, name):
-        inst.then_inc(sem[name], 1)
-        cnt[name] += 1
-        return (name, cnt[name])
+    def task(q, name, fn, *deps):
+        tasks[name] = (q, fn, deps)
 
-    def wait(q, qn, *toks):
-        for name, n in toks:
-            if seen.get((qn, name), 0) < n:
-                q.wait_ge(sem[name], n)
-                seen[(qn, name)] = n
+    def line(q, names):
+        order[q] += names.split()
 
-    def v(inst_fn, *toks):
-        wait(V, "v", *toks)
-        return done(inst_fn(), "sv")
+    def emit():
+        token = dict(landed)
+        for q in "vapg":
+            n = 0
+            for name in order[q]:
+                if name[0] != "_":
+                    n += 1
+                    token[name] = ("s" + q, n)
+        for q in queue:
+            seen = {}
+            for name in order[q]:
+                kind, fn, deps = tasks[name]
+                for d in deps:
+                    s, n = token[d] if d in token else token[d[:-1]]
+                    if seen.get(s, 0) < n:
+                        queue[q].wait_ge(sem[s], n)
+                        seen[s] = n
+                inst = fn(q) if kind == "va" else fn()
+                if name[0] != "_":
+                    inst.then_inc(sem["s" + q], 1)
 
-    def a(inst_fn, *toks):
-        wait(A, "a", *toks)
-        return done(inst_fn(), "sa")
-
-    def gp(inst_fn, *toks):
-        wait(g, "g", *toks)
-        return done(inst_fn(), "sg")
-
-    def conv(out, lhs, rhs_of, start=True, lo=0, hi=16):
+    def conv(out, lhs_of, rhs_of, start=False, stop=True):
         inst = None
-        for i in range(lo, hi):
-            inst = P.matmul(out, lhs[:, 15 - i:143 - i], rhs_of(i), start and i == 0, i == 15)
+        for i in range(16):
+            inst = P.matmul(out, lhs_of(i), rhs_of(i), start and i == 0, stop and i == 15)
         return inst
+
+    def row(t, at=0):
+        return lambda i: t[:, at + 15 - i:at + 143 - i]
 
     ps = [T["ps%d" % k] for k in range(8)]
     peers = [r for r in range(N) if r != me]
     far = [r for r in peers if topo.die(T.cores[r]) != topo.die(core)]
     near = [r for r in peers if topo.die(T.cores[r]) == topo.die(core)]
-    fc = BC * min(far)
-    nc = BC * min(near + [me])
+    mine = me // 4
+    eng = topo.engines(core, T.cores[peers[0]])
 
-    def dst_id(r):
-        rid, pid, _ = topo.addr(T.cores[r])
-        return DstId(rid=rid, pnc=pid)
+    def send(group, src, dst, arrive, left):
+        trs = []
+        for n_, r in enumerate(group):
+            rid, pid, _ = topo.addr(T.cores[r])
+            mask = sum(1 << e for e in eng[4 * n_:4 * n_ + 4])
+            trs.append(RemoteDMATransfer(dst_ids=[DstId(rid=rid, pnc=pid)], dma_engine_mask=mask, remote_sem=arrive,
+                                         src=src[:, CAP * r:CAP * r + CAP], dst=dst[:, CAP * me:CAP * me + CAP]))
+        return g.remote_dma_fused(trs, local_sem=left)
 
-    def bits(es):
-        m = 0
-        for e in es:
-            m |= 1 << e
-        return m
+    def dma(q, name, out, in_, s, *deps):
+        task(q, name, lambda: queue[q].dma_start(out, in_).then_inc(sem[s], 16), *deps)
 
-    Y.dma_start(T.ch[:], T.chunks[:]).then_inc(sem.l_ch, 16)
-    A.dma_start(T.wtc[:, 0:1], T.wt[:]).then_inc(sem.l_wt, 16)
-    Y.dma_start(T.di[:, 0:DH], T.head[:]).then_inc(sem.l_h, 16)
-    Y.dma_start(T.di[:, DH:DH + DV], T.vac[:]).then_inc(sem.l_fv, 16)
-    Y.dma_start(T.di[:, DH + DV:DD], T.follow[:]).then_inc(sem.l_fv, 16)
-    Y.dma_start(T.st[:, 0:S], T.store[:]).then_inc(sem.l_st, 16)
-    L_CH, L_WT, L_H, L_FV, L_ST = ("l_ch", 16), ("l_wt", 16), ("l_h", 16), ("l_fv", 32), ("l_st", 16)
+    st = T.st[:]
+    dma("a", "_wt", T.wr[0:1, :], T.wt[:], "l_wt")
+    dma("y", "_ch", T.ch[:], T.chunks[:], "l_ch")
+    dma("y", "_head", T.di[:, 0:DH], T.head[:], "l_h")
+    dma("y", "_follow", T.di[:, DH:DD], T.follow[:], "l_t")
+    dma("y", "_vac", T.vi[0:8, :], T.vac[:], "l_v")
+    dma("y", "_store", T.st[:, 0:S0], T.store[:, 0:S0], "l_st")
+    dma("y", "_store1", T.st[:, S0:S], T.store[:, S0:S], "l_st")
+    landed.update(WT=("l_wt", 16), CH=("l_ch", 16), HEAD=("l_h", 16), FOLLOW=("l_t", 16), VAC=("l_v", 16), ST=("l_st", 32), ZS=("l_z", 16),
+                  ROWS=("rows", 96), NEAR=("arr_near", 4 * len(near)), FAR=("arr_far", 4 * len(far)),
+                  ANS=("arr2", 4 * len(peers)), OY=("oy", 16), OZ=("oz", 16), S1=("snt1", 4 * len(peers)),
+                  S2=("snt2", 4 * len(peers)))
+    line("y", "_ch _head _follow _vac _store")
 
     fl = {"allow_small_or_imprecise_dtypes": True}
-    g_k = gp(lambda: g.iota(T.ki[:, 0:1], [[0, 1]], 0, 1))
-    g_u = gp(lambda: g.iota(T.u[:], [[1, 144]], 0, 0, **fl))
-    g_kf = gp(lambda: g.iota(T.kf[:, 0:1], [[0, 1]], 0, 1, **fl))
-    g_n1 = gp(lambda: g.iota(T.neg1[:], [[0, 128]], -1, 0, **fl))
-    g_p2 = gp(lambda: g.affine_select(T.p2n[:], T.neg1[:], [[16, 8], [0, 16]], Op.is_ge, 0.0, 15, -1), g_n1)
-    g_nu = gp(lambda: g.affine_select(T.negu[:], T.p2n[:], [[-1, 128]], Op.is_ge, 0.0, 0, 1), g_p2)
-    g_nb = gp(lambda: g.affine_select(T.negb[:], T.p2n[:], [[-16, 8], [0, 16]], Op.is_ge, 0.0, 0, 1))
-    g_wz = gp(lambda: g.iota(T.w[:, 0:MISS], [[0, MISS]], 0, 0, **fl))
-    g_nc = gp(lambda: g.iota(T.nc0[:], [[-16, 3 * C_]], -MISS, 0, **fl))
-    g_zc = gp(lambda: g.iota(T.w[:, WW:WW + 16], [[0, 16]], 0, 0, **fl))
+    task("g", "ki", lambda: g.iota(T.ki[:, 0:1], [[0, 1]], 0, 1))
+    task("g", "u", lambda: g.iota(T.u[:], [[1, 144]], 0, 0, **fl))
+    task("g", "kf", lambda: g.iota(T.kf[:, 0:1], [[0, 1]], 0, 1, **fl))
+    task("g", "ones", lambda: g.iota(T.ones[:], [[0, 128]], 1, 0, **fl))
+    task("g", "b1", lambda: g.affine_select(T.b1[:], T.ones[:], [[16, 8], [0, 16]], Op.is_ge, 0.0, 15, -1), "ones")
+    task("g", "blk", lambda: g.affine_select(T.blk[:], T.b1[:], [[-16, 8], [0, 16]], Op.is_ge, 0.0, 0, 1), "b1")
+    task("g", "low", lambda: g.affine_select(T.low[:], T.blk[:], [[1, 128]], Op.is_gt, 0.0, 0, -1), "blk")
+    task("g", "lift", lambda: g.affine_select(T.lift[:], T.low[:], [[1, 128]], Op.not_equal, BIG, 0, -1), "low")
+    task("g", "id0", lambda: g.iota(T.idf[:], [[64, DF // 64], [0, 64]], 0, DF, **fl))
+    task("g", "id1", lambda: g.iota(T.lo[:, 0:DF], [[0, DF // 64], [1, 64]], 0, 0, **fl))
+    task("g", "nc0", lambda: g.iota(T.nc0[:], [[-16, HC], [-H_, 4]], H_ - MISS, 0, **fl))
+    task("g", "la", lambda: g.affine_select(T.la[0:8, :], T.ones[0:8, :], [[1, 128]], Op.is_equal, 0.0, -1, -16))
+    task("g", "lb", lambda: g.affine_select(T.lb[0:8, :], T.ones[0:8, :], [[1, 128]], Op.is_equal, 0.0, 0, -16))
+    line("g", "ki u kf ones b1 blk low lift id0 id1 la lb nc0 ncy")
 
-    v_tz = v(lambda: V.memset(T.tb[:, 0:2048], 0.0))
-    v_g = v(lambda: V.tensor_scalar(T.ci[:, 0:1], T.ki[:, 0:1], 112, None, Op.bitwise_and), g_k)
-    v_sb = v(lambda: V.memset(T.sb[:], 0.0))
-    v_gf = v(lambda: V.tensor_scalar(T.cf[:, 0:1], T.ci[:, 0:1], 15.0, None, Op.add), v_g)
-    v_r1 = v(lambda: V.memset(T.rm[:], 1.0))
-    v_id = v(lambda: V.tensor_scalar(T.ident[:], T.u[:, 0:128], T.kf[:, 0:1], None, Op.is_equal), g_kf)
-    v_rm = v(lambda: V.memset(T.rm[:, 0:512:64], 0.0), v_r1)
-    v_wh = v(lambda: V.tensor_scalar(T.wh[:], T.u[:], T.cf[:, 0:1], T.wtc[:, 0:1], Op.is_equal, Op.mult), v_gf, L_WT)
-    v_sel = v(lambda: V.tensor_scalar(T.sel[:], T.u[:], T.cf[:, 0:1], None, Op.is_equal))
-    v_ni = v(lambda: V.tensor_scalar(T.negi[:], T.u[:, 0:128], T.kf[:, 0:1], -1.0, Op.is_equal, Op.mult))
+    cf = lambda k: T.cf[:, k:k + 1]
+    task("v", "tz0", lambda: V.memset(T.tb[:, 0:512], 0.0))
+    task("v", "one", lambda: V.memset(T.kf[:, 4:5], 1.0))
+    task("v", "grp", lambda: V.tensor_scalar(T.ci[:, 0:1], T.ki[:, 0:1], 112, None, Op.bitwise_and), "ki")
+    task("v", "sbz", lambda: V.memset(T.sb[:], 0.0))
+    task("v", "g15", lambda: V.tensor_scalar(cf(0), T.ci[:, 0:1], 15.0, None, Op.add), "grp")
+    task("v", "rm1", lambda: V.memset(T.rm[:], 1.0))
+    task("v", "r81", lambda: V.memset(T.r8[:], -float(CAP)))
+    task("v", "wh", lambda: V.tensor_scalar(T.wh[:], T.u[:], cf(0), ps[7][:, 0:1], Op.is_equal, Op.mult), "g15", "u", "wcol")
+    task("v", "ident", lambda: V.tensor_scalar(T.ident[:], T.u[:, 0:128], T.kf[:, 0:1], None, Op.is_equal), "kf")
+    task("v", "negi", lambda: V.tensor_scalar(T.negi[:], T.u[:, 0:128], T.kf[:, 0:1], -1.0, Op.is_equal, Op.mult))
+    task("v", "rm0", lambda: V.memset(T.rm[:, 0:N * EP:EP], 0.0), "rm1")
+    task("v", "e0", lambda: V.memset(T.e1[:, 0:N * EP:EP], 0.0))
+    task("v", "r80", lambda: V.memset(T.r8[:, 0:512:8], -65536.0), "r81")
+    task("v", "r", lambda: V.tensor_scalar(T.ci[:, 4:5], T.ki[:, 0:1], 15, None, Op.bitwise_and))
+    task("v", "odd", lambda: V.tensor_scalar(T.cj[:, 0:1], T.ki[:, 0:1], 1, None, Op.bitwise_and))
+    task("v", "pair", lambda: V.tensor_scalar(T.cj[:, 1:2], T.ki[:, 0:1], 1, 7, Op.arith_shift_right, Op.bitwise_and))
+    task("v", "rf", lambda: V.tensor_copy(cf(1), T.ci[:, 4:5]), "r")
+    task("v", "tz6", lambda: V.memset(T.tb[:, S - 512:S], 0.0))
+    task("v", "gS", lambda: V.tensor_scalar(cf(2), T.ci[:, 0:1], -float(DF), None, Op.mult))
+    line("v", "tz0 one grp sbz g15 gS rm1 tz6 wh r81 ident negi rm0 e0 r80")
+    task("a", "tz1", lambda: A.activation(T.tb[:, 512:1024], T.tb[:, 0:512], Act.Copy), "tz0")
+    for k in (2, 3, 4):
+        task("a", "tz%d" % k, lambda k=k: A.activation(T.tb[:, 1024 * k - 1024:1024 * k], T.tb[:, 0:1024], Act.Copy), "tz1")
+    task("a", "pos3", lambda: A.activation(T.pos3[:], T.negi[:], Act.Copy, scale=-3.0), "negi")
+    task("a", "tz5", lambda: A.activation(T.tb[:, B:B + 512], T.tb[:, 0:512], Act.Copy))
+    line("a", "_wt tz1 tz2 tz3 tz4")
+    task("p", "wcol", lambda: P.matmul(ps[7][:, 0:1], T.wr[0:1, :], T.kf[0:1, 4:5], True, True), "WT", "one")
+    task("p", "_open", lambda: P.matmul(ps[6][:, 0:512], T.ones[:], T.sb[:, 0:512], True, False), "sbz", "ones")
 
-    a(lambda: A.activation(T.tb[:, 2048:4096], T.tb[:, 0:2048], Act.Copy), v_tz)
-    a(lambda: A.activation(T.tb[:, 4096:S], T.tb[:, 0:1024], Act.Copy))
-    a(lambda: A.activation(T.nid[:], T.ident[:], Act.Copy, scale=-1.0), v_id)
-    a_wn = a(lambda: A.activation(T.wn[:], T.sel[:], Act.Copy, scale=-8192.0), v_sel)
-
-    wait(P, "p", v_wh, L_CH)
-    p_h1 = done(conv(ps[5][:, 0:64], T.wh, lambda i: T.ch[:, i:M:16]), "sp")
-    v_t1 = v(lambda: V.tensor_scalar(T.t1[:], ps[5][:, 0:64], 13.0, None, Op.mult), p_h1)
-    v_o4 = v(lambda: V.tensor_scalar(T.o4[:], T.t1[:], 28, None, Op.bitwise_and), v_t1)
-    v_e = None
+    task("p", "h1", lambda: conv(ps[5][:, 0:64], row(T.wh), lambda i: T.ch[:, i:M:16], start=True), "wh", "CH")
+    task("v", "t1", lambda: V.tensor_scalar(T.t1[:], ps[5][:, 0:64], 13.0, None, Op.mult), "h1")
+    task("v", "o4", lambda: V.tensor_scalar(T.o4[:], T.t1[:], 28, None, Op.bitwise_and), "t1")
     for q in range(N):
-        v_e = v(lambda: V.tensor_scalar(T.e1[:, 64 * q:64 * q + 64], T.o4[:], float(4 * q), None, Op.is_equal), v_o4)
-    v_s1 = v(lambda: V.tensor_tensor_scan(T.s1[:], T.rm[:], T.e1[:], 0.0, Op.mult, Op.subtract), v_e, v_rm)
-    wait(P, "p", v_e, g_nu)
-    P.matmul(ps[6][:, 0:512], T.negu[:], T.e1[:], True, False)
-    wait(P, "p", v_s1, g_nb)
-    p_n1 = done(P.matmul(ps[6][:, 0:512], T.negb[:], T.s1[:], False, True), "sp")
-    v_o160 = v(lambda: V.tensor_scalar(T.o160[:], T.o4[:], 40.0, None, Op.mult))
-    v_d1 = v(lambda: V.tensor_copy(T.df[:, 0:DH], T.di[:, 0:DH]), L_H)
-    v_pr = v(lambda: V.tensor_tensor(T.pr[:], ps[6][:, 0:512], T.e1[:], Op.mult), p_n1)
-    wait(P, "p", v_o160, v_id)
-    P.matmul(ps[7][:, 0:64], T.ident[:], T.o160[:], True, False)
-    wait(P, "p", v_pr)
-    inst = None
-    for q in range(N):
-        inst = P.matmul(ps[7][:, 0:64], T.ident[:], T.pr[:, 64 * q:64 * q + 64], False, q == N - 1)
-    p_sum = done(inst, "sp")
-    v_d2 = v(lambda: V.tensor_copy(T.df[:, DH:DD], T.di[:, DH:DD]), L_FV)
-    v_pos = v(lambda: V.tensor_copy(T.pos[:], ps[7][:, 0:64]), p_sum)
-    v_sc0 = v(lambda: V.tensor_copy(T.sb[:].indirect(T.pos[:]), T.ch[:]), v_pos, v_sb)
+        task("v", "e%d_" % q, lambda q=q: V.tensor_scalar(T.e1[:, EP * q + 1:EP * q + EP], T.o4[:], float(4 * q), None,
+                                                           Op.is_equal), "o4")
+        task("p", "_tri%d" % q, lambda q=q: P.matmul(ps[6][:, q:512:8], T.lift[:], T.e1[:, EP * q + 1:EP * q + EP],
+                                                     False, False), "e%d_" % q, "lift")
+        task("p", ("" if q == N - 1 else "_") + "sum%d" % q,
+             lambda q=q: P.matmul(ps[6][:, q:512:8], T.blk[:], T.s1[:, EP * q:EP * q + EP - 1], False, q == N - 1),
+             "s1%d" % (q >= 5))
+    for k, (a, b) in enumerate(((0, 5), (5, N))):
+        task("v", "s1%d" % k, lambda a=a, b=b: V.tensor_tensor_scan(T.s1[:, EP * a:EP * b], T.rm[:, EP * a:EP * b],
+                                                                    T.e1[:, EP * a:EP * b], 0.0, Op.mult, Op.add),
+             "e%d_" % (b - 1), "rm0", "e0")
+    task("v", "dh", lambda: V.tensor_copy(T.lh[:], T.di[:, 0:DH]), "HEAD")
+    task("v", "df", lambda: V.tensor_copy(T.df[:], T.di[:, DH:DD]), "FOLLOW")
+    task("v", "px", lambda: V.tensor_tensor_scan(T.px[:], T.r8[:], ps[6][:, 0:512], 0.0, Op.add, Op.max), "sum7", "r80")
+    task("v", "pos", lambda: V.tensor_scalar(T.pos[:], T.px[:, 7:512:8], BIG - CAP * (N - 1), None, Op.subtract), "px")
+    task("v", "sc0", lambda: V.tensor_copy(T.sb[:].indirect(T.pos[:]), T.ch[:]), "pos", "sbz")
+    line("v", "t1 dh o4 df " + " ".join("e%d_" % q for q in range(N)) + " s10 s11 vf px r odd pos pair rf sc0")
+    line("p", "wcol _open h1 _tri0 _lf0 _tri1 _tri2 _tri3 _tri4 _lf1 _tri5 _tri6 _tri7 "
+         + " ".join("_sum%d" % q for q in range(N - 1)) + " sum7")
+    task("g", "_near", lambda: send(near, T.sb, T.rb, sem.arr_near, sem.snt1), "sc0")
+    task("g", "_far", lambda: send(far, T.sb, T.rb, sem.arr_far, sem.snt1))
+    line("g", "_near _far")
 
-    eng = topo.engines(core, T.cores[peers[0]])
-    ev, od = eng[0::2], eng[1::2]
-    tr = []
-    for n_, r in enumerate(far):
-        tr.append((r, ev[2 * n_:2 * n_ + 2]))
-    for n_, r in enumerate(near):
-        tr.append((r, od[2 * n_:2 * n_ + 2]))
-    wait(g, "g", v_sc0)
-    g.remote_dma_fused([RemoteDMATransfer(dst_ids=[dst_id(r)], dma_engine_mask=bits(es), remote_sem=sem.arr1,
-                                          src=T.sb[:, CAP * r:CAP * r + CAP], dst=T.rb[:, CAP * me:CAP * me + CAP])
-                        for r, es in tr], local_sem=sem.snt1)
-    ARR1 = ("arr1", 2 * len(peers))
+    task("a", "hi", lambda: A.activation(T.hi[:, DF:2 * DF], T.df[:], Act.Copy), "df")
+    task("a", "idh", lambda: A.activation(T.hi[:, 0:DF], T.idf[:], Act.Identity, bias=cf(2)), "id0")
+    for k in range(2):
+        task("p", "_lf%d" % k, lambda k=k: P.matmul(ps[3][:, DF // 2 * k:DF // 2 * (k + 1)], T.negi[:],
+                                                    T.df[:, DF // 2 * k:DF // 2 * (k + 1)], k == 0, False), "df")
+    task("p", "lf", lambda: P.matmul(ps[3][:, 0:DF], T.ident[:], T.hi[:, DF:2 * DF], False, True), "hi")
+    task("a", "lof", lambda: A.activation(T.lo[:, DF:2 * DF], ps[3][:, 0:DF], Act.Copy, scale=-1.0), "lf")
+    line("a", "hi tz5 idh lof")
+    line("p", "lf")
+    dma("y", "_r2", T.tb[2:128:16, :], T.hi[:, DF:2 * DF], "rows", "tz5", "tz6")
+    dma("y", "_r0", T.tb[0:128:16, :], T.hi[:, 0:DF], "rows", "idh")
+    dma("y", "_r1", T.tb[1:128:16, :], T.lo[:, 0:DF], "rows", "id1")
+    dma("y", "_r3", T.tb[3:128:16, :], T.lo[:, DF:2 * DF], "rows", "lof")
+    dma("y", "_r4", T.tb[4:128:16, :], T.hi[:, DF:2 * DF], "rows")
+    dma("y", "_r5", T.tb[5:128:16, :], T.lo[:, DF:2 * DF], "rows")
+    line("y", "_r2 _r4 _r0 _r1 _r3 _r5 _store1")
 
-    a_h1 = a(lambda: A.activation(T.hi[:, 0:DH], T.df[:, 0:DH], Act.Copy), v_d1)
-    a_h2 = a(lambda: A.activation(T.hi[:, DH:DD], T.df[:, DH:DD], Act.Copy), v_d2)
-    wait(P, "p", v_ni, a_h1)
-    P.matmul(ps[2][:, 0:DH], T.negi[:], T.df[:, 0:DH], True, False)
-    p_l1 = done(P.matmul(ps[2][:, 0:DH], T.ident[:], T.hi[:, 0:DH], False, True), "sp")
-    wait(P, "p", a_h2)
-    P.matmul(ps[3][:, 0:DD - DH], T.negi[:], T.df[:, DH:DD], True, False)
-    p_l2 = done(P.matmul(ps[3][:, 0:DD - DH], T.ident[:], T.hi[:, DH:DD], False, True), "sp")
-    a_l1 = a(lambda: A.activation(T.lo[:, 0:DH], ps[2][:, 0:DH], Act.Copy, scale=-1.0), p_l1)
-    a_l2 = a(lambda: A.activation(T.lo[:, DH:DD], ps[3][:, 0:DD - DH], Act.Copy, scale=-1.0), p_l2)
-    wait(Y, "y", a_h2, g_wz)
-    Y.dma_start(T.tb[0:128:16, 0:B], T.hi[:, 0:DH]).then_inc(sem.rl, 16)
-    Y.dma_start(T.tb[2:128:16, 0:S], T.hi[:, DH + DV:DD]).then_inc(sem.rl, 16)
-    Y.dma_start(T.w[0:128:16, 0:MISS], T.hi[:, DH:DH + DV]).then_inc(sem.rl, 16)
-    wait(Y, "y", a_l1)
-    Y.dma_start(T.tb[1:128:16, 0:B], T.lo[:, 0:DH]).then_inc(sem.rl, 16)
-    wait(Y, "y", a_l2)
-    Y.dma_start(T.tb[3:128:16, 0:S], T.lo[:, DH + DV:DD]).then_inc(sem.rl, 16)
-    Y.dma_start(T.w[1:128:16, 0:MISS], T.lo[:, DH:DH + DV]).then_inc(sem.rl, 16)
-    RL = ("rl", 96)
-    a_own = a(lambda: A.activation(T.rb[:, CAP * me:CAP * me + CAP], T.sb[:, CAP * me:CAP * me + CAP], Act.Copy), v_sc0)
+    u16 = T.u[:, 0:16]
+    task("v", "vf", lambda: V.tensor_copy(T.vf[0:8, :], T.vi[0:8, :]), "VAC")
+    task("v", "below", lambda: V.tensor_scalar(T.below[:], u16, cf(1), None, Op.is_gt), "rf")
+    task("v", "at", lambda: V.tensor_scalar(cf(4), cf(1), 6.0, float(S * me), Op.is_equal, Op.mult), "rf")
+    task("v", "w6", lambda: V.tensor_scalar(cf(5), T.below[:, 4:5], 2.0, T.below[:, 6:7], Op.mult, Op.subtract), "below")
+    task("v", "m23", lambda: V.tensor_scalar(cf(13), T.below[:, 4:5], T.below[:, 2:3], None, Op.subtract), "below")
+    task("v", "wy", lambda: V.tensor_scalar(cf(12), cf(1), 6.0, cf(5), Op.is_equal, Op.add), "w6")
+    task("v", "sel6", lambda: V.tensor_scalar(T.sel6[:], T.u[:], cf(0), cf(5), Op.is_equal, Op.mult), "w6")
+    task("v", "ncs", lambda: V.tensor_scalar(T.ncs[:, 0:4 * HC], T.nc0[:], cf(1), None, Op.subtract), "nc0", "rf")
+    task("v", "eps", lambda: V.tensor_scalar(T.eps[:], T.ncs[:, 1:4 * HC:4], float(WW - MISS), -1.0 / EPS, Op.subtract, Op.mult), "ncs")
+    task("v", "nc4", lambda: V.memset(T.ncs[:, 0:4 * HC:4], -EPS), "eps")
+    task("v", "sel", lambda: V.tensor_scalar(T.sel[:], T.u[:], cf(0), None, Op.is_equal))
+    task("v", "y4", lambda: V.tensor_scalar(cf(14), T.ci[:, 0:1], 0.25, 3.0, Op.mult, Op.add))
+    task("v", "dig", lambda: V.tensor_scalar(cf(8), T.cj[:, 0:1], 255.0, 1.0, Op.mult, Op.add), "odd")
+    task("v", "to0", lambda: V.tensor_scalar(cf(10), T.cj[:, 1:2], cf(0), -15.0, Op.add, Op.add), "pair")
+    task("v", "to1", lambda: V.tensor_scalar(cf(11), T.cj[:, 1:2], cf(0), -7.0, Op.add, Op.add), "pair")
+    task("v", "sely", lambda: V.tensor_scalar(T.sely[:], T.u[:, 0:48], cf(14), cf(12), Op.is_equal, Op.mult), "y4", "wy")
+    for k in range(2):
+        task("v", "pk%d" % k, lambda k=k: V.tensor_scalar(T.pk[:, 128 * k:128 * k + 128], T.u[:, 0:128], cf(10 + k), cf(8),
+                                                          Op.is_equal, Op.mult), "dig", "to%d" % k)
+        task("g", "wp%d" % k, lambda k=k: g.affine_select(T.wp[:, 144 * k:144 * k + 144], T.wn[:], [[1 - 2 * k, 144]], Op.is_ge,
+                                                          0.0, (-8, 7)[k], 2 * k - 1), "wn")
+    task("a", "vac", lambda: A.activation(T.w[:, 0:MISS], ps[7][:, 0:MISS], Act.Copy), "vc")
+    task("g", "ncy", lambda: g.iota(T.ncy[0:1, :], [[0, 4 * HC]], WY, 0, **fl))
+    task("p", "_offY", lambda: P.matmul(ps[3][:, 0:4 * HC], T.ones[0:1, :], T.ncy[0:1, :], False, False), "ncy")
+    task("a", "cap", lambda: A.activation(T.cap[:], T.idf[:], Act.Identity, bias=EPS, scale=0.0))
+    task("v", "s20", lambda: V.memset(T.s2[:, 0:1], 0.0))
+    task("v", "wz", lambda: [V.memset(T.w[:, WY * k + WW:WY * k + WH], 0.0) for k in range(2)][-1])
+    line("v", "sel wn ncs own below dig to0 to1 eps y4 at w6 m23 pk0 pk1 nc4 sel6 wy s20 wz pk2 sely")
+    task("g", "sel4", lambda: g.affine_select(T.sel4[:], T.sel[:], [[1, 144]], Op.is_ge, 0.0, -12, -1), "sel")
+    task("g", "sel01", lambda: g.affine_select(T.sel01[:], T.sel[:], [[1, 144]], Op.is_ge, 0.0, -14, -1))
+    task("g", "sel23", lambda: g.affine_select(T.sel23[:], T.sel4[:], [[-1, 144]], Op.is_ge, 0.0, 13, 1), "sel4")
+    line("g", "sel4 sel01 sel23 wp0 wp1")
+    task("a", "lc", lambda: A.activation(T.lc[0:8, :], T.la[0:8, :], Act.Copy, scale=-1.0), "lb")
+    task("v", "own", lambda: V.tensor_copy(T.rb[:, CAP * me:CAP * me + CAP], T.sb[:, CAP * me:CAP * me + CAP]), "sc0")
+    task("a", "vh", lambda: A.activation(T.vh[0:8, :], T.vf[0:8, :], Act.Copy), "vf")
+    task("v", "wn", lambda: V.tensor_scalar(T.wn[:], T.u[:], cf(0), -8192.0, Op.is_equal, Op.mult))
+    task("v", "pk2", lambda: V.tensor_scalar(T.pk[:, 256:512], T.pk[:, 0:256], -1.0, None, Op.mult), "pk0", "pk1")
+    task("p", "_va", lambda: P.matmul(ps[7][:, 0:MISS], T.la[0:8, :], T.vf[0:8, :], True, False), "vf", "la")
+    task("p", "_vb", lambda: P.matmul(ps[7][:, 0:MISS], T.lb[0:8, :], T.vh[0:8, :], False, False), "vh")
+    task("p", "vc", lambda: P.matmul(ps[7][:, 0:MISS], T.lc[0:8, :], T.vh[0:8, :], False, True))
+    line("a", "lc vh pos3 cap")
+    line("p", "_va _vb vc")
 
-    v_r = v(lambda: V.tensor_scalar(T.ci[:, 4:5], T.ki[:, 0:1], 15, None, Op.bitwise_and))
-    v_rf = v(lambda: V.tensor_copy(T.cf[:, 1:2], T.ci[:, 4:5]), v_r)
-    v(lambda: V.tensor_scalar(T.cf[:, 2:3], T.ci[:, 4:5], 2.0, None, Op.is_lt))
-    v(lambda: V.tensor_scalar(T.cf[:, 3:4], T.ci[:, 4:5], 2.0, None, Op.is_ge))
-    v(lambda: V.tensor_scalar(T.cf[:, 4:5], T.ci[:, 4:5], 4.0, float(S * me), Op.is_equal, Op.mult))
-    v_m4 = v(lambda: V.tensor_scalar(T.cf[:, 5:6], T.ci[:, 4:5], 4.0, None, Op.is_lt))
-    v(lambda: V.tensor_scalar(T.ncs[:], T.nc0[:], T.cf[:, 1:2], None, Op.subtract), v_rf, g_zc)
-    v(lambda: V.tensor_scalar(T.ndu[:], T.nc0[:, 0:C_], T.cf[:, 1:2], float(MISS - S), Op.subtract, Op.add))
-    v(lambda: V.tensor_scalar(T.sel4[:], T.u[:], T.cf[:, 0:1], T.cf[:, 5:6], Op.is_equal, Op.mult), v_m4)
-    mH, mF, bias = T.cf[:, 2:3], T.cf[:, 3:4], T.cf[:, 4:5]
-    st = T.st[:, 0:S]
+    for name, q, a, b in SECOND:
+        task(q, name, lambda q=q, a=a, b=b: (V.tensor_copy(T.tb2[:, 16 * a:16 * b], T.tb[:].indirect(T.lh[:, a:b])) if q == "v" else
+                                             A.activation(T.tb2[:, 16 * a:16 * b], T.tb[:].indirect(T.lh[:, a:b]), Act.Copy)), "ROWS", "dh")
+    line("v", " ".join(n for n, q, *_ in SECOND if q == "v"))
+    line("a", "P0 P1")
+    bias = cf(4)
 
-    wait(P, "p", a_own, ARR1)
-    p_h2 = done(conv(ps[5][:, 0:C_], T.wh, lambda i: T.rb[:, i:R_:16]), "sp")
-    v_t2 = v(lambda: V.tensor_scalar(T.t2[:], ps[5][:, 0:C_], 13.0, None, Op.mult), p_h2)
-    v_b2 = v(lambda: V.tensor_scalar(T.b2[:], T.t2[:], 5, B - 1, Op.arith_shift_right, Op.bitwise_and), v_t2)
-    v_l0 = v(lambda: V.tensor_copy(T.lu[:, 0:C_], T.b2[:]), v_b2)
+    def half(h):
+        x = "XY"[h]
+        c0, c1 = HC * h, HC * h + HC
+        hb, lb, mb = ps[5 + h], ps[h], ps[2 + h]
+        win = T.w[:, 0:WY * h + WH]
 
-    def gout(k, c0, c1):
-        return T.w[:, MISS + R_ * k + 16 * c0:MISS + R_ * k + 16 * c1]
+        def met(k, a, b, step=None, at=0):
+            w0 = WY * h + MISS + H_ * k - 16 * c0
+            return T.w[:, w0 + 16 * a + at:w0 + 16 * b:step]
 
-    def a_gather(k, c0, c1, width, mask, *toks):
-        return a(lambda: A.activation(gout(k, c0, c1), T.tb[:, 0:width].indirect(T.lu[:, C_ * k + c0:C_ * k + c1]),
-                                      Act.Copy, scale=mask), *toks)
+        task("p", "_eps" + x, lambda: P.matmul(hb[:, 0:HC], T.negi[:], T.eps[:], True, False), "eps")
+        task("p", "_idx" + x, lambda: P.matmul(mb[:, 0:4 * HC], T.negi[:], T.ncs[:], True, False), "nc4", "lof")
+        task("p", "h" + x, lambda: conv(hb[:, 0:HC], row(T.wh), lambda i: T.rb[:, 16 * c0 + i:16 * c1:16]),
+             *(("NEAR", "own") if h == mine else ("FAR",)))
+        task("v", "t" + x, lambda: V.tensor_scalar(T.t2[:, c0:c1], hb[:, 0:HC], 13.0, None, Op.mult), "h" + x)
+        task("v", "a" + x, lambda: V.tensor_scalar(T.b2[:, c0:c1], T.t2[:, c0:c1], 1, 16 * (DH - 1), Op.arith_shift_right,
+                                                   Op.bitwise_and), "t" + x)
+        task("v", "b" + x, lambda: V.tensor_scalar(T.b3[:, c0:c1], T.t2[:, c0:c1], 13, 15, Op.arith_shift_right,
+                                                   Op.bitwise_and), "t" + x)
+        task("v", "j" + x, lambda: V.tensor_tensor(T.b4[:, c0:c1], T.b2[:, c0:c1], T.b3[:, c0:c1], Op.add), "a" + x, "b" + x)
+        task("v", "l0" + x, lambda: V.tensor_copy(T.lu[:, c0:c1], T.b4[:, c0:c1]), "j" + x)
+        mm = T.cap[:, 4 * c0:4 * c1:4]
+        task("a", "mm" + x, lambda: A.activation(mm, hb[:, 0:HC], Act.Relu, bias=float(WY * h), scale=-EPS), "t" + x, "cap")
 
-    def v_head(c0, c1, *toks):
-        return v(lambda: V.tensor_scalar(gout(0, c0, c1), T.tb[:, 0:B].indirect(T.lu[:, c0:c1]), mH, None, Op.mult), *toks)
+        def pieces(name, fn, *deps):
+            for p, a, b in (("", c0, c1), ("a", c0, c0 + HC // 2), ("b", c0 + HC // 2, c1)):
+                task("va", name + p, lambda q, a=a, b=b: fn(q, a, b), *deps)
+            return name + "a", name + "b"
 
-    def p_list(k, h, *toks):
-        wait(P, "p", *toks)
-        b0 = MISS + R_ * k + H_ * h
-        return done(conv(ps[h][:, 0:40], T.sel, lambda i: T.w[:, b0 + i:b0 + H_:16]), "sp")
+        def pick(q, out, in_, scale=None, bias=None):
+            if scale is None and bias is None:
+                return V.tensor_copy(out, in_) if q == "v" else A.activation(out, in_, Act.Copy)
+            if q == "v":
+                return V.tensor_scalar(out, in_, bias if scale is None else scale, None, Op.add if scale is None else Op.mult)
+            if scale is None:
+                return A.activation(out, in_, Act.Identity, bias=bias)
+            return A.activation(out, in_, Act.Copy, scale=scale)
 
-    def v_list(k, h, tok):
-        c0 = C_ * (k + 1) + 40 * h
-        return v(lambda: V.tensor_copy(T.lu[:, c0:c0 + 40], ps[h][:, 0:40]), tok)
+        pieces("G0" + x, lambda q, a, b: pick(q, met(0, a, b), T.tb2[:].indirect(T.lu[:, a:b])),
+               "l0" + x, *(n for n, *_ in SECOND))
+        got2 = pieces("G2" + x, lambda q, a, b: pick(q, met(2, a, b), T.tb[:].indirect(T.lu[:, 2 * C_ + a:2 * C_ + b])), "l2" + x)
+        task("va", "W" + x, lambda q: pick(q, met(1, c0, c1), met(2, c0, c1), scale=cf(13)), *got2, "m23")
 
-    def v_cmp(k, c0, c1, *toks):
-        l0 = C_ * (k + 1)
-        b0 = R_ * k
-        return v(lambda: V.tensor_tensor(T.nq[:, b0 + 16 * c0:b0 + 16 * c1], st.indirect(T.lu[:, l0 + c0:l0 + c1]),
-                                         T.rb[:, 16 * c0:16 * c1], Op.not_equal), *toks)
+        def step(k):
+            l0, b0, name = C_ * k, R_ * (k - 1), "%d%s" % (k, x)
+            rows, got, bank, free = ((T.sel01, 0, lb, "t" + x), (T.sel23, 0, hb, "mm" + x), (T.sel23, 2, lb, "l1" + x))[k - 1]
+            task("p", "c" + name, lambda: conv(bank[:, 0:HC], row(rows), lambda i: met(got, c0, c1, 16, i), start=True),
+                 "G%d%sa" % (got, x), "G%d%sb" % (got, x), free, "sel23")
+            task("v", "l" + name, lambda: V.tensor_copy(T.lu[:, l0 + c0:l0 + c1], bank[:, 0:HC]), "c" + name)
+            match, slot = "m" + name, (1, 3, 2)[k - 1]
+            last = match == [n for n in ORDER[mine]["p"].split() if n[0] == "m" and n[2] == x][-1]
+            if k < 3 and "1" + x not in ON_SCALAR and "2" + x not in ON_SCALAR:
+                pieces("C" + name, lambda q, a, b: V.tensor_tensor(
+                    T.np[:, 16 * a:16 * b, k - 1], st.indirect(T.lu[:, l0 + a:l0 + b]), T.rb[:, 16 * a:16 * b],
+                    Op.not_equal), "l" + name, "ST")
+                task("p", match, lambda: conv(mb[:, 1:4 * HC:2], row(T.wn), lambda i: T.np[:, 16 * c0 + i:16 * c1:16, :], stop=last),
+                     *("C%d%s%s" % (j, x, p) for j in (1, 2) for p in "ab"))
+                return
+            if name not in ON_SCALAR:
+                seen = pieces("C" + name, lambda q, a, b: V.tensor_tensor(
+                    T.nq[:, b0 + 16 * a:b0 + 16 * b], st.indirect(T.lu[:, l0 + a:l0 + b]), T.rb[:, 16 * a:16 * b],
+                    Op.not_equal), "l" + name, "ST")
+                task("p", match, lambda: conv(mb[:, slot:4 * HC:4], row(T.wn), lambda i: T.nq[:, b0 + 16 * c0 + i:b0 + 16 * c1:16],
+                                              stop=last), *seen)
+                return
+            db, g0, n0 = ps[ON_SCALAR[name]][:, 0:H_ // 2], b0 + 16 * c0, H_ // 2 * (k // 3)
 
-    def p_match(k, *toks):
-        out = ps[2 + k][:, 0:C_]
-        P.matmul(out, T.negi[:], T.ncs[:, C_ * k:C_ * k + C_], True, False)
-        wait(P, "p", *toks)
-        b0 = R_ * k
-        return done(conv(out, T.wn, lambda i: T.nq[:, b0 + i:b0 + R_:16], start=False), "sp")
+            def diff(src, at, k0, first):
+                P.matmul(db, T.pk[:, 128 * k0:128 * k0 + 128], src[:, at:at + H_:2], first, False)
+                return P.matmul(db, T.pk[:, 128 * k0 + 128:128 * k0 + 256], src[:, at + 1:at + H_:2], False, not first)
+            task("a", "D" + name, lambda: A.activation(T.nq[:, g0:g0 + H_], st.indirect(T.lu[:, l0 + c0:l0 + c1]), Act.Copy),
+                 "l" + name, "ST")
+            task("p", "_r" + name, lambda: diff(T.rb, 16 * c0, 2, True), "pk2", "wp1", "t" + x,
+                 *(("vac",) if ON_SCALAR[name] == 7 else ()))
+            task("p", "d" + name, lambda: diff(T.nq, g0, 0, False), "D" + name)
+            task("a", "E" + name, lambda: A.activation(T.n3[:, n0:n0 + H_ // 2], db, Act.Abs), "d" + name)
+            task("p", match, lambda: conv(mb[:, slot:4 * HC:4], lambda i: row(T.wp, 144 * (i % 2))(i),
+                                          lambda i: T.n3[:, n0 + i // 2:n0 + H_ // 2:8], stop=last), "E" + name)
+        for k in (1, 2, 3):
+            step(k)
 
-    a_ha = a_gather(0, 0, 20, B, mH, v_l0, RL)
-    a_hb = a_gather(0, 56, 80, B, mH)
-    v_ha = v_head(20, 40, v_l0, RL)
-    v_hb = v_head(40, 56)
-    v_m0 = v(lambda: V.tensor_scalar(T.mm[:], T.t2[:], -32.0, float(WW), Op.mult, Op.add))
-    v_pz = v(lambda: V.tensor_scalar(T.pz[:], T.t2[:], 0.0, None, Op.is_equal))
-    p1a = p_list(0, 0, a_ha, v_ha)
-    p1b = p_list(0, 1, a_hb, v_hb)
-    l1a = v_list(0, 0, p1a)
-    c1a = v_cmp(0, 0, 40, l1a, L_ST, ARR1, a_own)
-    l1b = v_list(0, 1, p1b)
-    c1b = v_cmp(0, 40, 80, l1b)
-    f1a = a_gather(1, 0, 40, S, mF, l1a)
-    f1b = a_gather(1, 40, 80, S, mF, l1b)
-    p2a = p_list(1, 0, f1a)
-    p2b = p_list(1, 1, f1b)
-    x1 = p_match(0, c1b)
-    l2a = v_list(1, 0, p2a)
-    c2a = v_cmp(1, 0, 40, l2a)
-    l2b = v_list(1, 1, p2b)
-    c2b = v_cmp(1, 40, 80, l2b)
-    f2a = a_gather(2, 0, 40, S, mF, l2a)
-    f2b = a_gather(2, 40, 80, S, mF, l2b)
-    p3a = p_list(2, 0, f2a)
-    p3b = p_list(2, 1, f2b)
-    l3a = v_list(2, 0, p3a)
-    c3a = v_cmp(2, 0, 20, l3a)
-    l3b = v_list(2, 1, p3b)
-    c3b = v_cmp(2, 40, 80, l3b)
-    a_g3 = a(lambda: A.activation(T.g3[:], st.indirect(T.lu[:, 3 * C_ + 20:3 * C_ + 40]), Act.Copy), l3a)
-    wait(P, "p", a_g3)
-    P.matmul(ps[7][:, 0:320], T.nid[:], T.rb[:, 320:640], True, False)
-    p_d3 = done(P.matmul(ps[7][:, 0:320], T.ident[:], T.g3[:], False, True), "sp")
-    a_d3 = a(lambda: A.activation(T.nq[:, 2 * R_ + 320:2 * R_ + 640], ps[7][:, 0:320], Act.Abs), p_d3)
-    x2 = p_match(1, c2b)
-    x3 = p_match(2, a_d3, c3b)
+        mf = T.mf[:, 4 * c0 + 3:4 * c1:4]
+        task("v", "M" + x, lambda: V.tensor_tensor_scan(T.mf[:, 4 * c0:4 * c1], mb[:, 0:4 * HC], T.cap[:, 4 * c0:4 * c1], 0.0,
+                                                        Op.max, Op.min),
+             *(n for n in ORDER[mine]["p"].split() if n[0] == "m" and n[2] == x), "mm" + x)
+        task("v", "e" + x, lambda: V.tensor_scalar(T.e2[:, c0:c1], mf, 1.0, None, Op.is_lt), "M" + x)
+        task("v", "s" + x, lambda: V.tensor_tensor_scan(T.s2[:, c0 + 1:c1 + 1], T.e2[:, c0:c1], T.e2[:, c0:c1],
+                                                        T.s2[:, c0:c0 + 1], Op.add, Op.max), "e" + x, "sX" if h else "s20")
+        task("p", "_ra" + x, lambda: P.matmul(hb[:, 0:HC], T.low[:], T.e2[:, c0:c1], True, False), "e" + x)
+        task("p", "rb" + x, lambda: P.matmul(hb[:, 0:HC], T.blk[:], T.s2[:, c0:c1], False, True), "s" + x)
+        task("v", "x" + x, lambda: V.tensor_tensor(T.xf[:, c0:c1], hb[:, 0:HC], mf, Op.max), "rb" + x)
+        task("v", "i" + x, lambda: V.tensor_scalar(T.idx[:, c0:c1], T.xf[:, c0:c1], float(WW + WY * h), None, Op.min), "x" + x)
+        ans = pieces("A" + x, lambda q, a, b: pick(q, T.an[:, 16 * a:16 * b], win.indirect(T.idx[:, a:b]), bias=bias),
+                     "i" + x, "wz", "vac", "WX", "W" + x, "at")
+        task("p", "_tp" + x, lambda: P.matmul(lb[:, 0:HC], T.pos3[:], mm, True, False), "l3" + x, "sel6")
+        task("p", "ct" + x, lambda: conv(lb[:, 0:HC], row(T.sel6), lambda i: T.an[:, 16 * c0 + i:16 * c1:16]), *ans)
+        task("v", "T" + x, lambda: V.tensor_copy(T.tg[:, c0:c1], lb[:, 0:HC]), "ct" + x)
+        task("g", "_ans" + x, lambda: send([r for r in peers if r // 4 == h], T.an, T.ab, sem.arr2, sem.snt2), *ans)
+        if h == mine:
+            task("a", "ab", lambda: A.activation(T.ab[:, CAP * me:CAP * me + CAP], T.an[:, CAP * me:CAP * me + CAP], Act.Copy), *ans)
+    half(0)
+    half(1)
+    cut = FIRST[mine]
+    task("v", "SX", lambda: V.tensor_copy(T.zs[:].indirect(T.tg[:, 0:cut]), T.rb[:, 0:16 * cut]), "TX", "ZS")
+    task("v", "SY", lambda: V.tensor_copy(T.zs[:].indirect(T.tg[:, cut:C_]), T.rb[:, 16 * cut:R_]), "TY", "SX")
+    line("p", "_epsX _epsY _idxX _idxY _offY")
+    for q in "vap":
+        line(q, ORDER[mine][q])
+    line("g", "_ansX _ansY")
+    dma("y", "_zs", T.zs[:, 0:S], T.store[:], "l_z", "S1")
+    dma("y", "_z", T.z[:], T.zs[:, 0:S], "oz", "SY")
 
-    v_m1 = v(lambda: V.tensor_tensor(T.m3[:], ps[2][:, 0:C_], T.mm[:], Op.max), x1, v_m0)
-    v_np = v(lambda: V.tensor_tensor(T.npad[:], T.pz[:], T.ndu[:], Op.mult), v_pz)
-    v_m2 = v(lambda: V.tensor_tensor(T.mm[:], ps[3][:, 0:C_], T.m3[:], Op.max), x2, v_m1)
-    v_th = v(lambda: V.tensor_scalar(T.thr[:], T.mm[:], -100000.0, 0.0, Op.mult, Op.min), v_m2)
-    v_e2 = v(lambda: V.tensor_tensor(T.e2[:], ps[4][:, 0:C_], T.thr[:], Op.is_lt), x3, v_th)
-    v_s2 = v(lambda: V.tensor_tensor_scan(T.s2[:], T.e2[:], T.e2[:], 0.0, Op.min, Op.subtract), v_e2)
-    v_m3 = v(lambda: V.tensor_tensor(T.m3[:], ps[4][:, 0:C_], T.mm[:], Op.max))
-    wait(P, "p", v_e2)
-    P.matmul(ps[6][:, 0:C_], T.negu[:], T.e2[:], True, False)
-    wait(P, "p", v_s2)
-    p_n2 = done(P.matmul(ps[6][:, 0:C_], T.negb[:], T.s2[:], False, True), "sp")
-    v_xf = v(lambda: V.tensor_tensor(T.xf[:], ps[6][:, 0:C_], T.m3[:], Op.max), p_n2, v_m3)
-    v_ix = v(lambda: V.tensor_copy(T.idx[:], T.xf[:]), v_xf)
-
-    def a_ans(c0, c1, *toks):
-        return a(lambda: A.activation(T.an[:, 16 * c0:16 * c1], T.w[:].indirect(T.idx[:, c0:c1]), Act.Identity,
-                                      bias=bias), *toks)
-
-    def v_ans(c0, c1, *toks):
-        return v(lambda: V.tensor_scalar(T.an[:, 16 * c0:16 * c1], T.w[:].indirect(T.idx[:, c0:c1]), bias, None, Op.add),
-                 *toks)
-
-    def p_target(bank, c0, c1, *toks):
-        out = ps[bank][:, 0:c1 - c0]
-        P.matmul(out, T.negi[:], T.npad[:, c0:c1], True, False)
-        wait(P, "p", *toks)
-        return done(conv(out, T.sel4, lambda i: T.an[:, 16 * c0 + i:16 * c1:16], start=False), "sp")
-
-    def v_fill(bank, c0, c1, tok, *prev):
-        t = v(lambda: V.tensor_copy(T.tg[:, c0:c1], ps[bank][:, 0:c1 - c0]), tok)
-        return v(lambda: V.tensor_copy(T.st[:].indirect(T.tg[:, c0:c1]), T.rb[:, 16 * c0:16 * c1]), t, *prev)
-
-    def send_answers(grp, *toks):
-        wait(g, "g", *toks)
-        g.remote_dma_fused([RemoteDMATransfer(dst_ids=[dst_id(r)], dma_engine_mask=bits(eng[4 * n_:4 * n_ + 4]),
-                                              remote_sem=sem.arr2, src=T.an[:, CAP * r:CAP * r + CAP],
-                                              dst=T.ab[:, CAP * me:CAP * me + CAP])
-                            for n_, r in enumerate(grp)], local_sem=sem.snt2)
-
-    a1 = a_ans(fc, fc + 8, v_ix, g_zc)
-    v1 = v_ans(fc + 8, fc + 16, v_ix)
-    a2 = a_ans(fc + 16, fc + 28)
-    v2 = v_ans(fc + 28, fc + 40)
-    a3 = a_ans(nc, nc + 40)
-    a_ab = a(lambda: A.activation(T.ab[:, CAP * me:CAP * me + CAP], T.an[:, CAP * me:CAP * me + CAP], Act.Copy), a3)
-    send_answers(far, a2, v2)
-    send_answers(near, a3)
-    ARR2 = ("arr2", 4 * len(peers))
-    t1_ = p_target(0, fc, fc + 16, a1, v1)
-    t2_ = p_target(1, fc + 16, fc + 40, a2, v2)
-    t3_ = p_target(2, nc, nc + 40, a3)
-    s1_ = v_fill(0, fc, fc + 16, t1_)
-    s2_ = v_fill(1, fc + 16, fc + 40, t2_, s1_)
-    s3_ = v_fill(2, nc, nc + 40, t3_, s2_)
-    wait(Y, "y", s3_)
-    Y.dma_start(T.z[:], st).then_inc(sem.oz, 16)
-
-    ya = []
-    for c0, c1 in ((0, 16), (16, 32)):
-        ya.append(a(lambda: A.activation(T.yg[:, 16 * c0:16 * c1], T.ab[:].indirect(T.pos[:, c0:c1]), Act.Copy),
-                    a_ab, ARR2))
-    yv = v(lambda: V.tensor_copy(T.yg[:, 512:M], T.ab[:].indirect(T.pos[:, 32:64])), a_ab, ARR2)
-    rhs_y = lambda i: T.yg[:, 64 * i:64 * i + 64]
-    wait(P, "p", ya[0])
-    conv(ps[5][:, 0:64], T.sel, rhs_y, lo=0, hi=4)
-    wait(P, "p", ya[1])
-    conv(ps[5][:, 0:64], T.sel, rhs_y, lo=4, hi=8)
-    wait(P, "p", yv)
-    p_y = done(conv(ps[5][:, 0:64], T.sel, rhs_y, lo=8, hi=16), "sp")
-    a_y = a(lambda: A.activation(T.ys[:], ps[5][:, 0:64], Act.Copy), p_y)
-    wait(A, "a", a_y)
-    A.dma_start(T.y[:], T.ys[:]).then_inc(sem.oy, 16)
-    A.wait_ge(sem.oy, 16)
-    Y.wait_ge(sem.oz, 16)
-    g.wait_ge(sem.snt1, 2 * len(peers))
-    g.wait_ge(sem.snt2, 4 * len(peers))
+    task("a", "ya", lambda: A.activation(T.yg[:, 0:512], T.ab[:].indirect(T.pos[:, 0:32]), Act.Copy), "ab", "ANS")
+    task("va", "yv", lambda q: (V.tensor_copy(T.yg[:, 512:M], T.ab[:].indirect(T.pos[:, 32:64])) if q == "v" else
+                                A.activation(T.yg[:, 512:M], T.ab[:].indirect(T.pos[:, 32:64]), Act.Copy)), "ab", "ANS")
+    for i in range(4):
+        task("p", ("" if i == 3 else "_") + "y%d" % i, lambda i=i: P.matmul(
+            ps[4][0:32, 0:256], T.sely[:, 3 - i:35 - i], T.yg[:, 256 * i:256 * i + 256], i == 0, i == 3), "ya" if i < 2 else "yv")
+    task("a", "ys", lambda: A.activation(T.ys[0:32, :], ps[4][0:32, 0:256], Act.Copy), "y3")
+    dma("a", "_y", T.y[:], T.ys[0:32, :], "oy", "ys")
+    task("a", "_endy", lambda: None, "OY")
+    task("y", "_endz", lambda: None, "OZ")
+    task("g", "_end", lambda: None, "S1", "S2")
+    line("a", "ya")
+    line(YV, "yv")
+    line("a", "ys _y _endy")
+    line("p", "_y0 _y1 _y2 y3")
+    line("y", "_zs _z _endz")
+    line("g", "_end")
+    emit()

from concourse.bass import DstId, RemoteDMATransfer
from concourse.mybir import AluOpType as Op, ActivationFunctionType as Act

N, M, S, B, CAP, MISS = 8, 1024, 5120, 4096, 160, 512
R_ = N * CAP
C_ = R_ // 16
H_ = R_ // 2
HC = C_ // 2
WW = MISS + 3 * H_
WH = WW + 16
WY = WH - MISS
DH, DF = B // 16, S // 16
DD = DH + DF
S0 = 3072
EP = M // 16 + 1
BIG = 2048.0
EPS = 2.0 ** 19

SCRATCH = {
    "ch": ("sbuf", [128, M], "bfloat16"),
    "wr": ("sbuf", [128, 128], "float32"),
    "st": ("sbuf", [128, S], "bfloat16"),
    "zs": ("sbuf", [128, 3 * (WW + WY + H_)], "bfloat16"),
    "tb": ("sbuf", [128, S], "bfloat16"),
    "tb2": ("sbuf", [128, B], "bfloat16"),
    "lh": ("sbuf", [128, DH], "uint16"),
    "di": ("sbuf", [128, DD], "int32"),
    "df": ("sbuf", [128, DF], "float32"),
    "idf": ("sbuf", [128, DF], "float32"),
    "hi": ("sbuf", [128, 2 * DF], "bfloat16"),
    "lo": ("sbuf", [128, 2 * DF], "bfloat16"),
    "b3": ("sbuf", [128, C_], "int32"),
    "b4": ("sbuf", [128, C_], "float32"),
    "vi": ("sbuf", [128, MISS], "int32"),
    "vf": ("sbuf", [128, MISS], "float32"),
    "vh": ("sbuf", [128, MISS], "bfloat16"),
    "la": ("sbuf", [128, 128], "float32"),
    "lb": ("sbuf", [128, 128], "bfloat16"),
    "lc": ("sbuf", [128, 128], "bfloat16"),
    "sb": ("sbuf", [128, R_], "bfloat16"),
    "rb": ("sbuf", [128, R_], "bfloat16"),
    "w": ("sbuf", [128, WH + WY], "bfloat16"),
    "nq": ("sbuf", [128, 3 * R_], "bfloat16"),
    "n3": ("sbuf", [128, H_], "bfloat16"),
    "an": ("sbuf", [128, R_], "bfloat16"),
    "ab": ("sbuf", [128, R_], "bfloat16"),
    "yg": ("sbuf", [128, M], "bfloat16"),
    "ys": ("sbuf", [128, 256], "float32"),
    "ki": ("sbuf", [128, 8], "int32"),
    "kf": ("sbuf", [128, 8], "float32"),
    "ci": ("sbuf", [128, 8], "int32"),
    "cj": ("sbuf", [128, 8], "int32"),
    "cf": ("sbuf", [128, 16], "float32"),
    "below": ("sbuf", [128, 16], "float32"),
    "u": ("sbuf", [128, 144], "float32"),
    "ones": ("sbuf", [128, 128], "bfloat16"),
    "b1": ("sbuf", [128, 128], "bfloat16"),
    "blk": ("sbuf", [128, 128], "bfloat16"),
    "low": ("sbuf", [128, 128], "bfloat16"),
    "lift": ("sbuf", [128, 128], "bfloat16"),
    "ident": ("sbuf", [128, 128], "bfloat16"),
    "negi": ("sbuf", [128, 128], "float32"),
    "pos3": ("sbuf", [128, 128], "float32"),
    "pk": ("sbuf", [128, 512], "bfloat16"),
    "sel": ("sbuf", [128, 144], "bfloat16"),
    "sel4": ("sbuf", [128, 144], "bfloat16"),
    "sel6": ("sbuf", [128, 144], "bfloat16"),
    "sel01": ("sbuf", [128, 144], "bfloat16"),
    "sel23": ("sbuf", [128, 144], "bfloat16"),
    "sely": ("sbuf", [128, 48], "bfloat16"),
    "wh": ("sbuf", [128, 144], "bfloat16"),
    "wn": ("sbuf", [128, 144], "bfloat16"),
    "wp": ("sbuf", [128, 288], "bfloat16"),
    "rm": ("sbuf", [128, N * EP], "bfloat16"),
    "r8": ("sbuf", [128, 512], "bfloat16"),
    "cap": ("sbuf", [128, 4 * C_], "float32"),
    "np": ("sbuf", [128, R_, 2], "bfloat16"),
    "nc0": ("sbuf", [128, 4 * HC], "float32"),
    "ncs": ("sbuf", [128, 4 * HC], "float32"),
    "ncy": ("sbuf", [128, 4 * HC], "bfloat16"),
    "eps": ("sbuf", [128, HC], "float32"),
    "t1": ("sbuf", [128, 64], "int32"),
    "o4": ("sbuf", [128, 64], "int32"),
    "e1": ("sbuf", [128, N * EP], "bfloat16"),
    "s1": ("sbuf", [128, N * EP], "bfloat16"),
    "px": ("sbuf", [128, 512], "float32"),
    "pos": ("sbuf", [128, 64], "uint16"),
    "t2": ("sbuf", [128, C_], "int32"),
    "b2": ("sbuf", [128, C_], "int32"),
    "lu": ("sbuf", [128, 4 * C_], "uint16"),
    "mf": ("sbuf", [128, 4 * C_], "float32"),
    "e2": ("sbuf", [128, C_], "bfloat16"),
    "s2": ("sbuf", [128, C_ + 8], "bfloat16"),
    "xf": ("sbuf", [128, C_], "float32"),
    "idx": ("sbuf", [128, C_], "uint16"),
    "tg": ("sbuf", [128, C_], "uint16"),
}
for _k in range(8):
    SCRATCH["ps%d" % _k] = ("psum", [128, 512], "float32")

SEMAPHORES = ["sv", "sa", "sp", "sg", "l_ch", "l_wt", "l_h", "l_t", "l_v", "l_st", "l_z", "rows",
              "arr_near", "arr_far", "snt1", "arr2", "snt2", "oz", "oy"]

YV = "v"
FIRST = {0: 40, 1: 40}
BY_SCALAR = {0: {"1Y": 7, "3Y": 4}, 1: {"1Y": 4, "3Y": 7}}
ORDER = {
    0: {"v": "tX bX aX jX tY l0X aY bY G0Xb jY l0Y G0Yb l2X l1X C1Xa l2Y C1Xb C2Xb l1Y l3X C2Xa C3Xa l3Y C3Xb C2Ya WX "
             "MX eX sX C2Yb xX iX AXb MY eY sY TX xY iY SX TY SY",
        "a": "mmX G0Xa mmY vac G0Ya G2X G2Y D1Y D3Y E1Y E3Y AXa WY ab AY",
        "p": "hX hY c2X c1X c2Y _r1Y c1Y c3X _r3Y c3Y m2X d1Y m3X d3Y m1Y _raX _tpX rbX m3Y m2Y ctX _tpY _raY rbY ctY"},
    1: {"v": "tY bY aY jY tX l0Y bX aX G0Ya jX l0X G0Xa l2Y C2Y l2X l1Y l1X C2X C1Xb l3Y C1Xa l3X C3X "
             "MX eX sX WX MY xX eY iX sY AXb xY iY TX SX TY SY",
        "a": "mmY G0Yb mmX vac G0Xb G2Y G2X D1Y D3Y E1Y E3Y WY AXa AY ab",
        "p": "hY hX _r1Y c2Y c1Y c2X c1X _r3Y c3Y c3X m2Y d1Y m2X d3Y m3X m1Y m3Y _raX rbX _tpX _raY rbY ctX _tpY ctY"},
}
SECOND = (("P0", "a", 0, 96), ("P1", "a", 96, 200), ("P3", "v", 200, 256))


def rank_program(g, core, T, topo):
    me = T.rank_of(core)
    if me is None:
        return
    ON_SCALAR = BY_SCALAR[me // 4]
    sem = T.sem
    V, A, P, Y = g.vector, g.scalar, g.tensor, g.sync
    queue = {"v": V, "a": A, "p": P, "g": g, "y": Y}
    tasks, order = {}, {q: [] for q in queue}
    landed = {}

    def task(q, name, fn, *deps):
        tasks[name] = (q, fn, deps)

    def line(q, names):
        order[q] += names.split()

    def emit():
        token = dict(landed)
        for q in "vapg":
            n = 0
            for name in order[q]:
                if name[0] != "_":
                    n += 1
                    token[name] = ("s" + q, n)
        for q in queue:
            seen = {}
            for name in order[q]:
                kind, fn, deps = tasks[name]
                for d in deps:
                    s, n = token[d] if d in token else token[d[:-1]]
                    if seen.get(s, 0) < n:
                        queue[q].wait_ge(sem[s], n)
                        seen[s] = n
                inst = fn(q) if kind == "va" else fn()
                if name[0] != "_":
                    inst.then_inc(sem["s" + q], 1)

    def conv(out, lhs_of, rhs_of, start=False, stop=True):
        inst = None
        for i in range(16):
            inst = P.matmul(out, lhs_of(i), rhs_of(i), start and i == 0, stop and i == 15)
        return inst

    def row(t, at=0):
        return lambda i: t[:, at + 15 - i:at + 143 - i]

    ps = [T["ps%d" % k] for k in range(8)]
    peers = [r for r in range(N) if r != me]
    far = [r for r in peers if topo.die(T.cores[r]) != topo.die(core)]
    near = [r for r in peers if topo.die(T.cores[r]) == topo.die(core)]
    mine = me // 4
    eng = topo.engines(core, T.cores[peers[0]])

    def send(group, src, dst, arrive, left):
        trs = []
        for n_, r in enumerate(group):
            rid, pid, _ = topo.addr(T.cores[r])
            mask = sum(1 << e for e in eng[4 * n_:4 * n_ + 4])
            trs.append(RemoteDMATransfer(dst_ids=[DstId(rid=rid, pnc=pid)], dma_engine_mask=mask, remote_sem=arrive,
                                         src=src[:, CAP * r:CAP * r + CAP], dst=dst[:, CAP * me:CAP * me + CAP]))
        return g.remote_dma_fused(trs, local_sem=left)

    def dma(q, name, out, in_, s, *deps):
        task(q, name, lambda: queue[q].dma_start(out, in_).then_inc(sem[s], 16), *deps)

    st = T.st[:]
    dma("a", "_wt", T.wr[0:1, :], T.wt[:], "l_wt")
    dma("y", "_ch", T.ch[:], T.chunks[:], "l_ch")
    dma("y", "_head", T.di[:, 0:DH], T.head[:], "l_h")
    dma("y", "_follow", T.di[:, DH:DD], T.follow[:], "l_t")
    dma("y", "_vac", T.vi[0:8, :], T.vac[:], "l_v")
    dma("y", "_store", T.st[:, 0:S0], T.store[:, 0:S0], "l_st")
    dma("y", "_store1", T.st[:, S0:S], T.store[:, S0:S], "l_st")
    landed.update(WT=("l_wt", 16), CH=("l_ch", 16), HEAD=("l_h", 16), FOLLOW=("l_t", 16), VAC=("l_v", 16), ST=("l_st", 32), ZS=("l_z", 16),
                  ROWS=("rows", 96), NEAR=("arr_near", 4 * len(near)), FAR=("arr_far", 4 * len(far)),
                  ANS=("arr2", 4 * len(peers)), OY=("oy", 16), OZ=("oz", 16), S1=("snt1", 4 * len(peers)),
                  S2=("snt2", 4 * len(peers)))
    line("y", "_ch _head _follow _vac _store")

    fl = {"allow_small_or_imprecise_dtypes": True}
    task("g", "ki", lambda: g.iota(T.ki[:, 0:1], [[0, 1]], 0, 1))
    task("g", "u", lambda: g.iota(T.u[:], [[1, 144]], 0, 0, **fl))
    task("g", "kf", lambda: g.iota(T.kf[:, 0:1], [[0, 1]], 0, 1, **fl))
    task("g", "ones", lambda: g.iota(T.ones[:], [[0, 128]], 1, 0, **fl))
    task("g", "b1", lambda: g.affine_select(T.b1[:], T.ones[:], [[16, 8], [0, 16]], Op.is_ge, 0.0, 15, -1), "ones")
    task("g", "blk", lambda: g.affine_select(T.blk[:], T.b1[:], [[-16, 8], [0, 16]], Op.is_ge, 0.0, 0, 1), "b1")
    task("g", "low", lambda: g.affine_select(T.low[:], T.blk[:], [[1, 128]], Op.is_gt, 0.0, 0, -1), "blk")
    task("g", "lift", lambda: g.affine_select(T.lift[:], T.low[:], [[1, 128]], Op.not_equal, BIG, 0, -1), "low")
    task("g", "id0", lambda: g.iota(T.idf[:], [[64, DF // 64], [0, 64]], 0, DF, **fl))
    task("g", "id1", lambda: g.iota(T.lo[:, 0:DF], [[0, DF // 64], [1, 64]], 0, 0, **fl))
    task("g", "nc0", lambda: g.iota(T.nc0[:], [[-16, HC], [-H_, 4]], H_ - MISS, 0, **fl))
    task("g", "la", lambda: g.affine_select(T.la[0:8, :], T.ones[0:8, :], [[1, 128]], Op.is_equal, 0.0, -1, -16))
    task("g", "lb", lambda: g.affine_select(T.lb[0:8, :], T.ones[0:8, :], [[1, 128]], Op.is_equal, 0.0, 0, -16))
    line("g", "ki u kf ones b1 blk low lift id0 id1 la lb nc0 ncy")

    cf = lambda k: T.cf[:, k:k + 1]
    task("v", "tz0", lambda: V.memset(T.tb[:, 0:512], 0.0))
    task("v", "one", lambda: V.memset(T.kf[:, 4:5], 1.0))
    task("v", "grp", lambda: V.tensor_scalar(T.ci[:, 0:1], T.ki[:, 0:1], 112, None, Op.bitwise_and), "ki")
    task("v", "sbz", lambda: V.memset(T.sb[:], 0.0))
    task("v", "g15", lambda: V.tensor_scalar(cf(0), T.ci[:, 0:1], 15.0, None, Op.add), "grp")
    task("v", "rm1", lambda: V.memset(T.rm[:], 1.0))
    task("v", "r81", lambda: V.memset(T.r8[:], -float(CAP)))
    task("v", "wh", lambda: V.tensor_scalar(T.wh[:], T.u[:], cf(0), ps[7][:, 0:1], Op.is_equal, Op.mult), "g15", "u", "wcol")
    task("v", "ident", lambda: V.tensor_scalar(T.ident[:], T.u[:, 0:128], T.kf[:, 0:1], None, Op.is_equal), "kf")
    task("v", "negi", lambda: V.tensor_scalar(T.negi[:], T.u[:, 0:128], T.kf[:, 0:1], -1.0, Op.is_equal, Op.mult))
    task("v", "rm0", lambda: V.memset(T.rm[:, 0:N * EP:EP], 0.0), "rm1")
    task("v", "e0", lambda: V.memset(T.e1[:, 0:N * EP:EP], 0.0))
    task("v", "r80", lambda: V.memset(T.r8[:, 0:512:8], -65536.0), "r81")
    task("v", "r", lambda: V.tensor_scalar(T.ci[:, 4:5], T.ki[:, 0:1], 15, None, Op.bitwise_and))
    task("v", "odd", lambda: V.tensor_scalar(T.cj[:, 0:1], T.ki[:, 0:1], 1, None, Op.bitwise_and))
    task("v", "pair", lambda: V.tensor_scalar(T.cj[:, 1:2], T.ki[:, 0:1], 1, 7, Op.arith_shift_right, Op.bitwise_and))
    task("v", "rf", lambda: V.tensor_copy(cf(1), T.ci[:, 4:5]), "r")
    task("v", "tz6", lambda: V.memset(T.tb[:, S - 512:S], 0.0))
    task("v", "gS", lambda: V.tensor_scalar(cf(2), T.ci[:, 0:1], -float(DF), None, Op.mult))
    line("v", "tz0 one grp sbz g15 gS rm1 tz6 wh r81 ident negi rm0 e0 r80")
    task("a", "tz1", lambda: A.activation(T.tb[:, 512:1024], T.tb[:, 0:512], Act.Copy), "tz0")
    for k in (2, 3, 4):
        task("a", "tz%d" % k, lambda k=k: A.activation(T.tb[:, 1024 * k - 1024:1024 * k], T.tb[:, 0:1024], Act.Copy), "tz1")
    task("a", "pos3", lambda: A.activation(T.pos3[:], T.negi[:], Act.Copy, scale=-3.0), "negi")
    task("a", "tz5", lambda: A.activation(T.tb[:, B:B + 512], T.tb[:, 0:512], Act.Copy))
    line("a", "_wt tz1 tz2 tz3 tz4")
    task("p", "wcol", lambda: P.matmul(ps[7][:, 0:1], T.wr[0:1, :], T.kf[0:1, 4:5], True, True), "WT", "one")
    task("p", "_open", lambda: P.matmul(ps[6][:, 0:512], T.ones[:], T.sb[:, 0:512], True, False), "sbz", "ones")

    task("p", "h1", lambda: conv(ps[5][:, 0:64], row(T.wh), lambda i: T.ch[:, i:M:16], start=True), "wh", "CH")
    task("v", "t1", lambda: V.tensor_scalar(T.t1[:], ps[5][:, 0:64], 13.0, None, Op.mult), "h1")
    task("v", "o4", lambda: V.tensor_scalar(T.o4[:], T.t1[:], 28, None, Op.bitwise_and), "t1")
    for q in range(N):
        task("v", "e%d_" % q, lambda q=q: V.tensor_scalar(T.e1[:, EP * q + 1:EP * q + EP], T.o4[:], float(4 * q), None,
                                                           Op.is_equal), "o4")
        task("p", "_tri%d" % q, lambda q=q: P.matmul(ps[6][:, q:512:8], T.lift[:], T.e1[:, EP * q + 1:EP * q + EP],
                                                     False, False), "e%d_" % q, "lift")
        task("p", ("" if q == N - 1 else "_") + "sum%d" % q,
             lambda q=q: P.matmul(ps[6][:, q:512:8], T.blk[:], T.s1[:, EP * q:EP * q + EP - 1], False, q == N - 1),
             "s1%d" % (q >= 5))
    for k, (a, b) in enumerate(((0, 5), (5, N))):
        task("v", "s1%d" % k, lambda a=a, b=b: V.tensor_tensor_scan(T.s1[:, EP * a:EP * b], T.rm[:, EP * a:EP * b],
                                                                    T.e1[:, EP * a:EP * b], 0.0, Op.mult, Op.add),
             "e%d_" % (b - 1), "rm0", "e0")
    task("v", "dh", lambda: V.tensor_copy(T.lh[:], T.di[:, 0:DH]), "HEAD")
    task("v", "df", lambda: V.tensor_copy(T.df[:], T.di[:, DH:DD]), "FOLLOW")
    task("v", "px", lambda: V.tensor_tensor_scan(T.px[:], T.r8[:], ps[6][:, 0:512], 0.0, Op.add, Op.max), "sum7", "r80")
    task("v", "pos", lambda: V.tensor_scalar(T.pos[:], T.px[:, 7:512:8], BIG - CAP * (N - 1), None, Op.subtract), "px")
    task("v", "sc0", lambda: V.tensor_copy(T.sb[:].indirect(T.pos[:]), T.ch[:]), "pos", "sbz")
    line("v", "t1 dh o4 df " + " ".join("e%d_" % q for q in range(N)) + " s10 s11 vf px r odd pos pair rf sc0")
    line("p", "wcol _open h1 _tri0 _lf0 _tri1 _tri2 _tri3 _tri4 _lf1 _tri5 _tri6 _tri7 "
         + " ".join("_sum%d" % q for q in range(N - 1)) + " sum7")
    task("g", "_near", lambda: send(near, T.sb, T.rb, sem.arr_near, sem.snt1), "sc0")
    task("g", "_far", lambda: send(far, T.sb, T.rb, sem.arr_far, sem.snt1))
    line("g", "_near _far")

    task("a", "hi", lambda: A.activation(T.hi[:, DF:2 * DF], T.df[:], Act.Copy), "df")
    task("a", "idh", lambda: A.activation(T.hi[:, 0:DF], T.idf[:], Act.Identity, bias=cf(2)), "id0")
    for k in range(2):
        task("p", "_lf%d" % k, lambda k=k: P.matmul(ps[3][:, DF // 2 * k:DF // 2 * (k + 1)], T.negi[:],
                                                    T.df[:, DF // 2 * k:DF // 2 * (k + 1)], k == 0, False), "df")
    task("p", "lf", lambda: P.matmul(ps[3][:, 0:DF], T.ident[:], T.hi[:, DF:2 * DF], False, True), "hi")
    task("a", "lof", lambda: A.activation(T.lo[:, DF:2 * DF], ps[3][:, 0:DF], Act.Copy, scale=-1.0), "lf")
    line("a", "hi tz5 idh lof")
    line("p", "lf")
    dma("y", "_r2", T.tb[2:128:16, :], T.hi[:, DF:2 * DF], "rows", "tz5", "tz6")
    dma("y", "_r0", T.tb[0:128:16, :], T.hi[:, 0:DF], "rows", "idh")
    dma("y", "_r1", T.tb[1:128:16, :], T.lo[:, 0:DF], "rows", "id1")
    dma("y", "_r3", T.tb[3:128:16, :], T.lo[:, DF:2 * DF], "rows", "lof")
    dma("y", "_r4", T.tb[4:128:16, :], T.hi[:, DF:2 * DF], "rows")
    dma("y", "_r5", T.tb[5:128:16, :], T.lo[:, DF:2 * DF], "rows")
    line("y", "_r2 _r4 _r0 _r1 _r3 _r5 _store1")

    u16 = T.u[:, 0:16]
    task("v", "vf", lambda: V.tensor_copy(T.vf[0:8, :], T.vi[0:8, :]), "VAC")
    task("v", "below", lambda: V.tensor_scalar(T.below[:], u16, cf(1), None, Op.is_gt), "rf")
    task("v", "at", lambda: V.tensor_scalar(cf(4), cf(1), 6.0, float(S * me), Op.is_equal, Op.mult), "rf")
    task("v", "w6", lambda: V.tensor_scalar(cf(5), T.below[:, 4:5], 2.0, T.below[:, 6:7], Op.mult, Op.subtract), "below")
    task("v", "m23", lambda: V.tensor_scalar(cf(13), T.below[:, 4:5], T.below[:, 2:3], None, Op.subtract), "below")
    task("v", "wy", lambda: V.tensor_scalar(cf(12), cf(1), 6.0, cf(5), Op.is_equal, Op.add), "w6")
    task("v", "sel6", lambda: V.tensor_scalar(T.sel6[:], T.u[:], cf(0), cf(5), Op.is_equal, Op.mult), "w6")
    task("v", "ncs", lambda: V.tensor_scalar(T.ncs[:, 0:4 * HC], T.nc0[:], cf(1), None, Op.subtract), "nc0", "rf")
    task("v", "eps", lambda: V.tensor_scalar(T.eps[:], T.ncs[:, 1:4 * HC:4], float(WW - MISS), -1.0 / EPS, Op.subtract, Op.mult), "ncs")
    task("v", "nc4", lambda: V.memset(T.ncs[:, 0:4 * HC:4], -EPS), "eps")
    task("v", "sel", lambda: V.tensor_scalar(T.sel[:], T.u[:], cf(0), None, Op.is_equal))
    task("v", "y4", lambda: V.tensor_scalar(cf(14), T.ci[:, 0:1], 0.25, 3.0, Op.mult, Op.add))
    task("v", "dig", lambda: V.tensor_scalar(cf(8), T.cj[:, 0:1], 255.0, 1.0, Op.mult, Op.add), "odd")
    task("v", "to0", lambda: V.tensor_scalar(cf(10), T.cj[:, 1:2], cf(0), -15.0, Op.add, Op.add), "pair")
    task("v", "to1", lambda: V.tensor_scalar(cf(11), T.cj[:, 1:2], cf(0), -7.0, Op.add, Op.add), "pair")
    task("v", "sely", lambda: V.tensor_scalar(T.sely[:], T.u[:, 0:48], cf(14), cf(12), Op.is_equal, Op.mult), "y4", "wy")
    for k in range(2):
        task("v", "pk%d" % k, lambda k=k: V.tensor_scalar(T.pk[:, 128 * k:128 * k + 128], T.u[:, 0:128], cf(10 + k), cf(8),
                                                          Op.is_equal, Op.mult), "dig", "to%d" % k)
        task("g", "wp%d" % k, lambda k=k: g.affine_select(T.wp[:, 144 * k:144 * k + 144], T.wn[:], [[1 - 2 * k, 144]], Op.is_ge,
                                                          0.0, (-8, 7)[k], 2 * k - 1), "wn")
    task("a", "vac", lambda: A.activation(T.w[:, 0:MISS], ps[7][:, 0:MISS], Act.Copy), "vc")
    task("g", "ncy", lambda: g.iota(T.ncy[0:1, :], [[0, 4 * HC]], WY, 0, **fl))
    task("p", "_offY", lambda: P.matmul(ps[3][:, 0:4 * HC], T.ones[0:1, :], T.ncy[0:1, :], False, False), "ncy")
    task("a", "cap", lambda: A.activation(T.cap[:], T.idf[:], Act.Identity, bias=EPS, scale=0.0))
    task("v", "s20", lambda: V.memset(T.s2[:, 0:1], 0.0))
    task("v", "wz", lambda: [V.memset(T.w[:, WY * k + WW:WY * k + WH], 0.0) for k in range(2)][-1])
    line("v", "sel wn ncs own below dig to0 to1 eps y4 at w6 m23 pk0 pk1 nc4 sel6 wy s20 wz pk2 sely")
    task("g", "sel4", lambda: g.affine_select(T.sel4[:], T.sel[:], [[1, 144]], Op.is_ge, 0.0, -12, -1), "sel")
    task("g", "sel01", lambda: g.affine_select(T.sel01[:], T.sel[:], [[1, 144]], Op.is_ge, 0.0, -14, -1))
    task("g", "sel23", lambda: g.affine_select(T.sel23[:], T.sel4[:], [[-1, 144]], Op.is_ge, 0.0, 13, 1), "sel4")
    line("g", "sel4 sel01 sel23 wp0 wp1")
    task("a", "lc", lambda: A.activation(T.lc[0:8, :], T.la[0:8, :], Act.Copy, scale=-1.0), "lb")
    task("v", "own", lambda: V.tensor_copy(T.rb[:, CAP * me:CAP * me + CAP], T.sb[:, CAP * me:CAP * me + CAP]), "sc0")
    task("a", "vh", lambda: A.activation(T.vh[0:8, :], T.vf[0:8, :], Act.Copy), "vf")
    task("v", "wn", lambda: V.tensor_scalar(T.wn[:], T.u[:], cf(0), -8192.0, Op.is_equal, Op.mult))
    task("v", "pk2", lambda: V.tensor_scalar(T.pk[:, 256:512], T.pk[:, 0:256], -1.0, None, Op.mult), "pk0", "pk1")
    task("p", "_va", lambda: P.matmul(ps[7][:, 0:MISS], T.la[0:8, :], T.vf[0:8, :], True, False), "vf", "la")
    task("p", "_vb", lambda: P.matmul(ps[7][:, 0:MISS], T.lb[0:8, :], T.vh[0:8, :], False, False), "vh")
    task("p", "vc", lambda: P.matmul(ps[7][:, 0:MISS], T.lc[0:8, :], T.vh[0:8, :], False, True))
    line("a", "lc vh pos3 cap")
    line("p", "_va _vb vc")

    for name, q, a, b in SECOND:
        task(q, name, lambda q=q, a=a, b=b: (V.tensor_copy(T.tb2[:, 16 * a:16 * b], T.tb[:].indirect(T.lh[:, a:b])) if q == "v" else
                                             A.activation(T.tb2[:, 16 * a:16 * b], T.tb[:].indirect(T.lh[:, a:b]), Act.Copy)), "ROWS", "dh")
    line("v", " ".join(n for n, q, *_ in SECOND if q == "v"))
    line("a", "P0 P1")
    bias = cf(4)

    def half(h):
        x = "XY"[h]
        c0, c1 = HC * h, HC * h + HC
        hb, lb, mb = ps[5 + h], ps[h], ps[2 + h]
        win = T.w[:, 0:WY * h + WH]

        def met(k, a, b, step=None, at=0):
            w0 = WY * h + MISS + H_ * k - 16 * c0
            return T.w[:, w0 + 16 * a + at:w0 + 16 * b:step]

        task("p", "_eps" + x, lambda: P.matmul(hb[:, 0:HC], T.negi[:], T.eps[:], True, False), "eps")
        task("p", "_idx" + x, lambda: P.matmul(mb[:, 0:4 * HC], T.negi[:], T.ncs[:], True, False), "nc4", "lof")
        task("p", "h" + x, lambda: conv(hb[:, 0:HC], row(T.wh), lambda i: T.rb[:, 16 * c0 + i:16 * c1:16]),
             *(("NEAR", "own") if h == mine else ("FAR",)))
        task("v", "t" + x, lambda: V.tensor_scalar(T.t2[:, c0:c1], hb[:, 0:HC], 13.0, None, Op.mult), "h" + x)
        task("v", "a" + x, lambda: V.tensor_scalar(T.b2[:, c0:c1], T.t2[:, c0:c1], 1, 16 * (DH - 1), Op.arith_shift_right,
                                                   Op.bitwise_and), "t" + x)
        task("v", "b" + x, lambda: V.tensor_scalar(T.b3[:, c0:c1], T.t2[:, c0:c1], 13, 15, Op.arith_shift_right,
                                                   Op.bitwise_and), "t" + x)
        task("v", "j" + x, lambda: V.tensor_tensor(T.b4[:, c0:c1], T.b2[:, c0:c1], T.b3[:, c0:c1], Op.add), "a" + x, "b" + x)
        task("v", "l0" + x, lambda: V.tensor_copy(T.lu[:, c0:c1], T.b4[:, c0:c1]), "j" + x)
        mm = T.cap[:, 4 * c0:4 * c1:4]
        task("a", "mm" + x, lambda: A.activation(mm, hb[:, 0:HC], Act.Relu, bias=float(WY * h), scale=-EPS), "t" + x, "cap")

        def pieces(name, fn, *deps):
            for p, a, b in (("", c0, c1), ("a", c0, c0 + HC // 2), ("b", c0 + HC // 2, c1)):
                task("va", name + p, lambda q, a=a, b=b: fn(q, a, b), *deps)
            return name + "a", name + "b"

        def pick(q, out, in_, scale=None, bias=None):
            if scale is None and bias is None:
                return V.tensor_copy(out, in_) if q == "v" else A.activation(out, in_, Act.Copy)
            if q == "v":
                return V.tensor_scalar(out, in_, bias if scale is None else scale, None, Op.add if scale is None else Op.mult)
            if scale is None:
                return A.activation(out, in_, Act.Identity, bias=bias)
            return A.activation(out, in_, Act.Copy, scale=scale)

        pieces("G0" + x, lambda q, a, b: pick(q, met(0, a, b), T.tb2[:].indirect(T.lu[:, a:b])),
               "l0" + x, *(n for n, *_ in SECOND))
        got2 = pieces("G2" + x, lambda q, a, b: pick(q, met(2, a, b), T.tb[:].indirect(T.lu[:, 2 * C_ + a:2 * C_ + b])), "l2" + x)
        task("va", "W" + x, lambda q: pick(q, met(1, c0, c1), met(2, c0, c1), scale=cf(13)), *got2, "m23")

        def step(k):
            l0, b0, name = C_ * k, R_ * (k - 1), "%d%s" % (k, x)
            rows, got, bank, free = ((T.sel01, 0, lb, "t" + x), (T.sel23, 0, hb, "mm" + x), (T.sel23, 2, lb, "l1" + x))[k - 1]
            task("p", "c" + name, lambda: conv(bank[:, 0:HC], row(rows), lambda i: met(got, c0, c1, 16, i), start=True),
                 "G%d%sa" % (got, x), "G%d%sb" % (got, x), free, "sel23")
            task("v", "l" + name, lambda: V.tensor_copy(T.lu[:, l0 + c0:l0 + c1], bank[:, 0:HC]), "c" + name)
            match, slot = "m" + name, (1, 3, 2)[k - 1]
            last = match == [n for n in ORDER[mine]["p"].split() if n[0] == "m" and n[2] == x][-1]
            if k < 3 and "1" + x not in ON_SCALAR and "2" + x not in ON_SCALAR:
                pieces("C" + name, lambda q, a, b: V.tensor_tensor(
                    T.np[:, 16 * a:16 * b, k - 1], st.indirect(T.lu[:, l0 + a:l0 + b]), T.rb[:, 16 * a:16 * b],
                    Op.not_equal), "l" + name, "ST")
                task("p", match, lambda: conv(mb[:, 1:4 * HC:2], row(T.wn), lambda i: T.np[:, 16 * c0 + i:16 * c1:16, :], stop=last),
                     *("C%d%s%s" % (j, x, p) for j in (1, 2) for p in "ab"))
                return
            if name not in ON_SCALAR:
                seen = pieces("C" + name, lambda q, a, b: V.tensor_tensor(
                    T.nq[:, b0 + 16 * a:b0 + 16 * b], st.indirect(T.lu[:, l0 + a:l0 + b]), T.rb[:, 16 * a:16 * b],
                    Op.not_equal), "l" + name, "ST")
                task("p", match, lambda: conv(mb[:, slot:4 * HC:4], row(T.wn), lambda i: T.nq[:, b0 + 16 * c0 + i:b0 + 16 * c1:16],
                                              stop=last), *seen)
                return
            db, g0, n0 = ps[ON_SCALAR[name]][:, 0:H_ // 2], b0 + 16 * c0, H_ // 2 * (k // 3)

            def diff(src, at, k0, first):
                P.matmul(db, T.pk[:, 128 * k0:128 * k0 + 128], src[:, at:at + H_:2], first, False)
                return P.matmul(db, T.pk[:, 128 * k0 + 128:128 * k0 + 256], src[:, at + 1:at + H_:2], False, not first)
            task("a", "D" + name, lambda: A.activation(T.nq[:, g0:g0 + H_], st.indirect(T.lu[:, l0 + c0:l0 + c1]), Act.Copy),
                 "l" + name, "ST")
            task("p", "_r" + name, lambda: diff(T.rb, 16 * c0, 2, True), "pk2", "wp1", "t" + x,
                 *(("vac",) if ON_SCALAR[name] == 7 else ()))
            task("p", "d" + name, lambda: diff(T.nq, g0, 0, False), "D" + name)
            task("a", "E" + name, lambda: A.activation(T.n3[:, n0:n0 + H_ // 2], db, Act.Abs), "d" + name)
            task("p", match, lambda: conv(mb[:, slot:4 * HC:4], lambda i: row(T.wp, 144 * (i % 2))(i),
                                          lambda i: T.n3[:, n0 + i // 2:n0 + H_ // 2:8], stop=last), "E" + name)
        for k in (1, 2, 3):
            step(k)

        mf = T.mf[:, 4 * c0 + 3:4 * c1:4]
        task("v", "M" + x, lambda: V.tensor_tensor_scan(T.mf[:, 4 * c0:4 * c1], mb[:, 0:4 * HC], T.cap[:, 4 * c0:4 * c1], 0.0,
                                                        Op.max, Op.min),
             *(n for n in ORDER[mine]["p"].split() if n[0] == "m" and n[2] == x), "mm" + x)
        task("v", "e" + x, lambda: V.tensor_scalar(T.e2[:, c0:c1], mf, 1.0, None, Op.is_lt), "M" + x)
        task("v", "s" + x, lambda: V.tensor_tensor_scan(T.s2[:, c0 + 1:c1 + 1], T.e2[:, c0:c1], T.e2[:, c0:c1],
                                                        T.s2[:, c0:c0 + 1], Op.add, Op.max), "e" + x, "sX" if h else "s20")
        task("p", "_ra" + x, lambda: P.matmul(hb[:, 0:HC], T.low[:], T.e2[:, c0:c1], True, False), "e" + x)
        task("p", "rb" + x, lambda: P.matmul(hb[:, 0:HC], T.blk[:], T.s2[:, c0:c1], False, True), "s" + x)
        task("v", "x" + x, lambda: V.tensor_tensor(T.xf[:, c0:c1], hb[:, 0:HC], mf, Op.max), "rb" + x)
        task("v", "i" + x, lambda: V.tensor_scalar(T.idx[:, c0:c1], T.xf[:, c0:c1], float(WW + WY * h), None, Op.min), "x" + x)
        ans = pieces("A" + x, lambda q, a, b: pick(q, T.an[:, 16 * a:16 * b], win.indirect(T.idx[:, a:b]), bias=bias),
                     "i" + x, "wz", "vac", "WX", "W" + x, "at")
        task("p", "_tp" + x, lambda: P.matmul(lb[:, 0:HC], T.pos3[:], mm, True, False), "l3" + x, "sel6")
        task("p", "ct" + x, lambda: conv(lb[:, 0:HC], row(T.sel6), lambda i: T.an[:, 16 * c0 + i:16 * c1:16]), *ans)
        task("v", "T" + x, lambda: V.tensor_copy(T.tg[:, c0:c1], lb[:, 0:HC]), "ct" + x)
        task("g", "_ans" + x, lambda: send([r for r in peers if r // 4 == h], T.an, T.ab, sem.arr2, sem.snt2), *ans)
        if h == mine:
            task("a", "ab", lambda: A.activation(T.ab[:, CAP * me:CAP * me + CAP], T.an[:, CAP * me:CAP * me + CAP], Act.Copy), *ans)
    half(0)
    half(1)
    cut = FIRST[mine]
    task("v", "SX", lambda: V.tensor_copy(T.zs[:].indirect(T.tg[:, 0:cut]), T.rb[:, 0:16 * cut]), "TX", "ZS")
    task("v", "SY", lambda: V.tensor_copy(T.zs[:].indirect(T.tg[:, cut:C_]), T.rb[:, 16 * cut:R_]), "TY", "SX")
    line("p", "_epsX _epsY _idxX _idxY _offY")
    for q in "vap":
        line(q, ORDER[mine][q])
    line("g", "_ansX _ansY")
    dma("y", "_zs", T.zs[:, 0:S], T.store[:], "l_z", "S1")
    dma("y", "_z", T.z[:], T.zs[:, 0:S], "oz", "SY")

    task("a", "ya", lambda: A.activation(T.yg[:, 0:512], T.ab[:].indirect(T.pos[:, 0:32]), Act.Copy), "ab", "ANS")
    task("va", "yv", lambda q: (V.tensor_copy(T.yg[:, 512:M], T.ab[:].indirect(T.pos[:, 32:64])) if q == "v" else
                                A.activation(T.yg[:, 512:M], T.ab[:].indirect(T.pos[:, 32:64]), Act.Copy)), "ab", "ANS")
    for i in range(4):
        task("p", ("" if i == 3 else "_") + "y%d" % i, lambda i=i: P.matmul(
            ps[4][0:32, 0:256], T.sely[:, 3 - i:35 - i], T.yg[:, 256 * i:256 * i + 256], i == 0, i == 3), "ya" if i < 2 else "yv")
    task("a", "ys", lambda: A.activation(T.ys[0:32, :], ps[4][0:32, 0:256], Act.Copy), "y3")
    dma("a", "_y", T.y[:], T.ys[0:32, :], "oy", "ys")
    task("a", "_endy", lambda: None, "OY")
    task("y", "_endz", lambda: None, "OZ")
    task("g", "_end", lambda: None, "S1", "S2")
    line("a", "ya")
    line(YV, "yv")
    line("a", "ys _y _endy")
    line("p", "_y0 _y1 _y2 y3")
    line("y", "_zs _z _endz")
    line("g", "_end")
    emit()
